import numpy as np
import ml_dtypes


def mxq(x, axis, fmt="e4m3"):
    dtype, down = {"e4m3": (ml_dtypes.float8_e4m3fn, 7), "e5m2": (ml_dtypes.float8_e5m2, 14)}[fmt]
    v = np.moveaxis(np.asarray(x, np.float32).astype(ml_dtypes.bfloat16).astype(np.float64), axis, -1)
    blocks = v.reshape(v.shape[:-1] + (-1, 32))
    amax = np.abs(blocks).max(-1, keepdims=True)
    byte = np.maximum(np.where(amax > 0, np.frexp(amax)[1] - 1 + 127, 0) - down, 1)
    scale = np.exp2(byte - 127.0)
    codes = (blocks / scale).astype(np.float32).astype(dtype).astype(np.float64)
    return np.moveaxis((codes * scale).reshape(v.shape), -1, axis)


WIDE = False


def mx_kscale(k):
    if not WIDE:
        return np.ones(k)
    levels = np.array([10, -10, 5, -5, 0])
    if k % 512:
        return np.exp2(np.random.permutation(np.resize(levels, k // 32))).repeat(32)
    a = np.empty((k // 512, 16))
    for p in range(k // 512):
        a[p, :8] = np.random.permutation(np.resize(levels, 8))
        for g in range(8):
            far = levels[np.abs(levels - a[p, g]) >= 10]
            a[p, g + 8] = far[np.random.randint(len(far))]
    return np.exp2(a.ravel()).repeat(32)


def f64(x):
    return np.asarray(x).astype(np.float64)


def striped(idx):
    return np.tile(idx.reshape(-1, 16).T, (8, 1)).astype(np.uint16)


def unstriped(offs):
    return offs[:16].T.reshape(-1).astype(np.int64)


def sigmoid(v):
    return 1.0 / (1.0 + np.exp(-np.maximum(v, -700.0)))


K, T, S, J, H, N = 1024, 1024, 512, 512, 512, 128


def setup_inputs():
    n = np.random.standard_normal
    s = mx_kscale(K)[:, None]
    u = mx_kscale(H)
    r = mx_kscale(J)[:, None]
    return {
        "xT": (n((K, T)) * s).astype(np.float32),
        "eT": (n((J, S)) * r).astype(np.float32),
        "w1": (n((K, H)) / np.sqrt(K) / s * u).astype(np.float32),
        "w3": (n((J, H)) / np.sqrt(J) / r).astype(np.float32),
        "w2": (n((H, N)) / np.sqrt(H) / u[:, None]).astype(np.float32),
        "offs": striped(np.random.permutation(T)[:S]),
    }


def reference(xT, eT, w1, w3, w2, offs):
    c = mxq(f64(w1), 0, "e4m3").T @ mxq(f64(xT)[:, unstriped(offs)], 0, "e4m3")
    z = c * sigmoid(mxq(f64(w3), 0, "e4m3").T @ mxq(f64(eT), 0, "e4m3"))
    return mxq(f64(w2), 0, "e4m3").T @ mxq(z, 0, "e4m3")

@@ -1,0 +1,224 @@
+from contextlib import ExitStack
+
+import concourse.mybir as mybir
+
+F32 = mybir.dt.float32
+BF16 = mybir.dt.bfloat16
+U32 = mybir.dt.uint32
+U16 = mybir.dt.uint16
+U8 = mybir.dt.uint8
+FP8X4 = mybir.dt.float8_e4m3fn_x4
+SIGMOID = mybir.ActivationFunctionType.Sigmoid
+MULT = mybir.AluOpType.mult
+
+K, T, S, J, H, N = 1024, 1024, 512, 512, 512, 128
+FLOPS = 2 * S * (K * H + J * H + H * N)
+
+P = 128
+PACK = 4
+K_PASS = P * PACK
+CHUNK = 128
+HALVES = (slice(0, 128),)
+
+X_SCALAR = (264, 264, 264, 264)
+W1_SCALAR = (92, 116)
+W3_SCALAR = 104
+E_SCALAR = (96, 160)
+W2_SCALAR = 0
+
+
+def tile_picked_schnet_sigmoid_e_kernel(tc, xT, eT, w1, w3, w2, offs, out):
+    nc = tc.nc
+
+    def rows_of_4(dram):
+        return dram.rearrange("(p j) w -> p j w", j=PACK)
+
+    def cast_columns(dst, src, width, scalar_width):
+        dst = dst.rearrange("p (c i) t -> p c t i", i=4)
+        src = src.rearrange("p t (c i) -> p c t i", i=4)
+        cut = scalar_width // 4
+        if cut > 0:
+            nc.scalar.copy(out=dst[:, :cut], in_=src[:, :cut])
+        if cut < width // 4:
+            nc.vector.tensor_copy(out=dst[:, cut:], in_=src[:, cut:])
+
+    def load(dram, shape, name):
+        raw = keep.tile(shape, F32, name=name, align_bytes=64)
+        nc.sync.dma_start(out=raw[:], in_=rows_of_4(dram))
+        return raw
+
+    with ExitStack() as ctx:
+        keep = ctx.enter_context(tc.tile_pool(name="keep", bufs=1))
+        psum = ctx.enter_context(tc.psum_pool(name="psum", bufs=1))
+        ring = ctx.enter_context(tc.psum_pool(name="ring", bufs=2))
+
+        offsets = keep.tile([P, S // 16], U16, name="offsets")
+        x_raw = [load(xT[:K_PASS, :], [P, PACK, T], "x_raw_0")]
+        nc.sync.dma_start(offsets[:], offs)
+        x_raw.append(load(xT[K_PASS:, :], [P, PACK, T], "x_raw_1"))
+        w1_raw = [load(w1[s * K_PASS : (s + 1) * K_PASS, :], [P, PACK, H], f"w1_raw_{s}") for s in range(2)]
+        w3_raw = load(w3, [P, PACK, H], "w3_raw")
+        e_raw = [load(eT[:, h * 256 : (h + 1) * 256], [P, PACK, 256], f"e_raw_{h}") for h in range(2)]
+        w2_raw = load(w2, [P, PACK, N], "w2_raw")
+
+        warm = keep.tile([P, 1], F32, name="warm")
+        nc.vector.memset(warm[:], 0.0)
+        nc.scalar.activation(out=warm[:], in_=warm[:], func=SIGMOID)
+
+        x_scales = keep.tile([P, T], U8, name="x_scales", align_bytes=64)
+        nc.gpsimd.memset(x_scales[:], 0)
+        g_scales = keep.tile([P, S], U8, name="g_scales", align_bytes=64)
+        x_codes = [keep.tile([P, T], U32, name=f"x_codes_{s}", align_bytes=64) for s in range(2)]
+        g_codes = [keep.tile([P, S], U32, name=f"g_codes_{s}", align_bytes=64) for s in range(2)]
+
+        def quantize_atoms(s):
+            grouped = keep.tile([P, T, PACK], BF16, name=f"x_grouped_{s}", align_bytes=64)
+            for h in range(2):
+                cols = slice(h * 512, (h + 1) * 512)
+                cast_columns(grouped[:, cols, :], x_raw[s][:, :, cols], 512, X_SCALAR[2 * s + h])
+            for h in range(2):
+                cols = slice(h * 512, (h + 1) * 512)
+                nc.vector.quantize_mx(
+                    out=x_codes[s][:, cols].bitcast(FP8X4),
+                    scales=x_scales[4 * s : P, cols],
+                    in_=grouped[:, cols, :].rearrange("p w t -> p (w t)"),
+                )
+
+        def gather_codes(s):
+            nc.vector.tensor_copy(out=g_codes[s][:], in_=x_codes[s][:].indirect(offsets[:]))
+
+        quantize_atoms(0)
+        gather_codes(0)
+        quantize_atoms(1)
+
+        def weights(raw, name, cut):
+            codes = keep.tile([P, H], U32, name=f"{name}_codes", align_bytes=64)
+            scales = keep.tile([P, H], U8, name=f"{name}_scales", align_bytes=64)
+            grouped = keep.tile([P, PACK, P, PACK], BF16, name=f"{name}_grouped", align_bytes=64)
+            dst = grouped[:].rearrange("p t m j -> p m j t")
+            src = raw[:].rearrange("p j (m t) -> p m j t", t=PACK)
+            nc.scalar.copy(out=dst[:, :cut], in_=src[:, :cut])
+            nc.vector.tensor_copy(out=dst[:, cut:], in_=src[:, cut:])
+            nc.vector.quantize_mx(
+                out=codes[:].bitcast(FP8X4), scales=scales[:], in_=grouped[:].rearrange("p t m j -> p (t m j)")
+            )
+            return codes, scales
+
+        w1_q = [weights(w1_raw[0], "w1_0", W1_SCALAR[0])]
+        nc.vector.tensor_copy(out=g_scales[:], in_=x_scales[:].indirect(offsets[:]))
+        gather_codes(1)
+        w1_q.append(weights(w1_raw[1], "w1_1", W1_SCALAR[1]))
+        w3_codes, w3_scales = weights(w3_raw, "w3", W3_SCALAR)
+
+        c_banks = {}
+
+        def product_c(n):
+            cols = slice(n * CHUNK, (n + 1) * CHUNK)
+            c_banks[n] = psum.tile([P, PACK, CHUNK], F32, name=f"c_{n}")
+            for t in range(PACK):
+                rows = slice(t * P, (t + 1) * P)
+                for s in range(2):
+                    nc.tensor.matmul_mx(
+                        out=c_banks[n][:, t, :],
+                        lhsT=w1_q[s][0][:, rows].bitcast(FP8X4),
+                        lhsT_scale=w1_q[s][1][:, rows],
+                        rhs=g_codes[s][:, cols].bitcast(FP8X4),
+                        rhs_scale=g_scales[4 * s : P, cols],
+                        start=(s == 0),
+                        stop=(s == 1),
+                    )
+
+        e_codes = [keep.tile([P, 256], U32, name=f"e_codes_{h}", align_bytes=64) for h in range(2)]
+        e_scales = [keep.tile([P, 256], U8, name=f"e_scales_{h}", align_bytes=64) for h in range(2)]
+
+        def edges(h):
+            grouped = keep.tile([P, 256, PACK], BF16, name=f"e_grouped_{h}", align_bytes=64)
+            cast_columns(grouped[:], e_raw[h][:], 256, E_SCALAR[h])
+            for q in range(2):
+                part = slice(q * CHUNK, (q + 1) * CHUNK)
+                nc.vector.quantize_mx(
+                    out=e_codes[h][:, part].bitcast(FP8X4),
+                    scales=e_scales[h][:, part],
+                    in_=grouped[:, part, :].rearrange("p w t -> p (w t)"),
+                )
+
+        gates = {}
+
+        def gate(n):
+            h, q = divmod(n, 2)
+            part = slice(q * CHUNK, (q + 1) * CHUNK)
+            f_bank = ring.tile([P, PACK, CHUNK], F32, name="f_bank")
+            for t in range(PACK):
+                rows = slice(t * P, (t + 1) * P)
+                nc.tensor.matmul_mx(
+                    out=f_bank[:, t, :],
+                    lhsT=w3_codes[:, rows].bitcast(FP8X4),
+                    lhsT_scale=w3_scales[:, rows],
+                    rhs=e_codes[h][:, part].bitcast(FP8X4),
+                    rhs_scale=e_scales[h][:, part],
+                    start=True,
+                    stop=True,
+                )
+            gates[n] = keep.tile([P, CHUNK, PACK], F32, name=f"gate_{n}", align_bytes=64)
+            for half in HALVES:
+                nc.scalar.activation(
+                    out=gates[n][:, half, :], in_=f_bank[:, :, half].rearrange("p t n -> p n t"), func=SIGMOID
+                )
+
+        z_codes = {}
+        z_scales = {}
+
+        def message(n):
+            z = keep.tile([P, CHUNK, PACK], BF16, name=f"z_{n}", align_bytes=64)
+            for half in HALVES:
+                nc.vector.tensor_tensor(
+                    out=z[:, half, :],
+                    in0=c_banks[n][:, :, half].rearrange("p t n -> p n t"),
+                    in1=gates[n][:, half, :],
+                    op=MULT,
+                )
+            z_codes[n] = keep.tile([P, CHUNK], U32, name=f"z_codes_{n}", align_bytes=64)
+            z_scales[n] = keep.tile([P, CHUNK], U8, name=f"z_scales_{n}", align_bytes=64)
+            nc.vector.quantize_mx(
+                out=z_codes[n][:].bitcast(FP8X4), scales=z_scales[n][:], in_=z[:].rearrange("p n t -> p (n t)")
+            )
+
+        w2_codes = keep.tile([P, N], U32, name="w2_codes", align_bytes=64)
+        w2_scales = keep.tile([P, N], U8, name="w2_scales", align_bytes=64)
+
+        def project(n):
+            o_bank = ring.tile([P, CHUNK], F32, name="o_bank")
+            nc.tensor.matmul_mx(
+                out=o_bank[:],
+                lhsT=w2_codes[:].bitcast(FP8X4),
+                lhsT_scale=w2_scales[:],
+                rhs=z_codes[n][:].bitcast(FP8X4),
+                rhs_scale=z_scales[n][:],
+                start=True,
+                stop=True,
+            )
+            result = keep.tile([P, CHUNK], F32, name=f"result_{n}")
+            nc.scalar.copy(out=result[:], in_=o_bank[:])
+            nc.sync.dma_start(out=out[:, n * CHUNK : (n + 1) * CHUNK], in_=result[:])
+
+        edges(0)
+        product_c(0)
+        product_c(1)
+        gate(0)
+        gate(1)
+        edges(1)
+        message(0)
+        w2_grouped = keep.tile([P, N, PACK], BF16, name="w2_grouped", align_bytes=64)
+        cast_columns(w2_grouped[:], w2_raw[:], N, W2_SCALAR)
+        nc.vector.quantize_mx(
+            out=w2_codes[:].bitcast(FP8X4), scales=w2_scales[:], in_=w2_grouped[:].rearrange("p w t -> p (w t)")
+        )
+        gate(2)
+        product_c(2)
+        message(1)
+        gate(3)
+        product_c(3)
+        message(2)
+        message(3)
+        for n in range(4):
+            project(n)

@@ -18,13 +18,14 @@ P = 128
 PACK = 4
 K_PASS = P * PACK
 CHUNK = 128
-HALVES = (slice(0, 128),)
 
-X_SCALAR = (264, 264, 264, 264)
-W1_SCALAR = (92, 116)
-W3_SCALAR = 104
-E_SCALAR = (96, 160)
+X_SCALAR = (336, 400, 760, 680)
+W1_SCALAR = (128, 76)
+W3_SCALAR = 44
+E_SCALAR = (128, 128, 0, 128)
 W2_SCALAR = 0
+C_BANK = ("bank_0", "bank_1", "bank_2", "bank_3")
+F_BANK = ("bank_4", "bank_5", "bank_6", "bank_7")
 
 
 def tile_picked_schnet_sigmoid_e_kernel(tc, xT, eT, w1, w3, w2, offs, out):
@@ -36,11 +37,11 @@ def tile_picked_schnet_sigmoid_e_kernel(tc, xT, eT, w1, w3, w2, offs, out):
     def cast_columns(dst, src, width, scalar_width):
         dst = dst.rearrange("p (c i) t -> p c t i", i=4)
         src = src.rearrange("p t (c i) -> p c t i", i=4)
-        cut = scalar_width // 4
+        cut = (width - scalar_width) // 4
         if cut > 0:
-            nc.scalar.copy(out=dst[:, :cut], in_=src[:, :cut])
+            nc.vector.tensor_copy(out=dst[:, :cut], in_=src[:, :cut])
         if cut < width // 4:
-            nc.vector.tensor_copy(out=dst[:, cut:], in_=src[:, cut:])
+            nc.scalar.copy(out=dst[:, cut:], in_=src[:, cut:])
 
     def load(dram, shape, name):
         raw = keep.tile(shape, F32, name=name, align_bytes=64)
@@ -50,12 +51,17 @@ def tile_picked_schnet_sigmoid_e_kernel(tc, xT, eT, w1, w3, w2, offs, out):
     with ExitStack() as ctx:
         keep = ctx.enter_context(tc.tile_pool(name="keep", bufs=1))
         psum = ctx.enter_context(tc.psum_pool(name="psum", bufs=1))
-        ring = ctx.enter_context(tc.psum_pool(name="ring", bufs=2))
 
         offsets = keep.tile([P, S // 16], U16, name="offsets")
-        x_raw = [load(xT[:K_PASS, :], [P, PACK, T], "x_raw_0")]
+        def load_pair(s, u):
+            raw = keep.tile([P, 2, T], F32, name=f"x_raw_{s}_{u}", align_bytes=64)
+            rows = xT[s * K_PASS : (s + 1) * K_PASS, :].rearrange("(p j) w -> p j w", j=PACK)
+            nc.sync.dma_start(out=raw[:], in_=rows[:, 2 * u : 2 * u + 2, :])
+            return raw
+
+        x_raw = [load_pair(0, 0)]
         nc.sync.dma_start(offsets[:], offs)
-        x_raw.append(load(xT[K_PASS:, :], [P, PACK, T], "x_raw_1"))
+        x_raw.extend([load_pair(0, 1), load_pair(1, 0), load_pair(1, 1)])
         w1_raw = [load(w1[s * K_PASS : (s + 1) * K_PASS, :], [P, PACK, H], f"w1_raw_{s}") for s in range(2)]
         w3_raw = load(w3, [P, PACK, H], "w3_raw")
         e_raw = [load(eT[:, h * 256 : (h + 1) * 256], [P, PACK, 256], f"e_raw_{h}") for h in range(2)]
@@ -65,31 +71,26 @@ def tile_picked_schnet_sigmoid_e_kernel(tc, xT, eT, w1, w3, w2, offs, out):
         nc.vector.memset(warm[:], 0.0)
         nc.scalar.activation(out=warm[:], in_=warm[:], func=SIGMOID)
 
-        x_scales = keep.tile([P, T], U8, name="x_scales", align_bytes=64)
-        nc.gpsimd.memset(x_scales[:], 0)
-        g_scales = keep.tile([P, S], U8, name="g_scales", align_bytes=64)
-        x_codes = [keep.tile([P, T], U32, name=f"x_codes_{s}", align_bytes=64) for s in range(2)]
         g_codes = [keep.tile([P, S], U32, name=f"g_codes_{s}", align_bytes=64) for s in range(2)]
+        g_scales_0 = keep.tile([P, S], U8, name="g_scales_0", align_bytes=64)
+        planes = keep.tile([P, S], U8, name="planes", align_bytes=64)
 
-        def quantize_atoms(s):
-            grouped = keep.tile([P, T, PACK], BF16, name=f"x_grouped_{s}", align_bytes=64)
-            for h in range(2):
-                cols = slice(h * 512, (h + 1) * 512)
-                cast_columns(grouped[:, cols, :], x_raw[s][:, :, cols], 512, X_SCALAR[2 * s + h])
-            for h in range(2):
-                cols = slice(h * 512, (h + 1) * 512)
-                nc.vector.quantize_mx(
-                    out=x_codes[s][:, cols].bitcast(FP8X4),
-                    scales=x_scales[4 * s : P, cols],
-                    in_=grouped[:, cols, :].rearrange("p w t -> p (w t)"),
-                )
+        def pick_atoms(s):
+            picked = keep.tile([P, S, 2], U32, name=f"picked_{s}", align_bytes=64)
+            for u in range(2):
+                pairs = keep.tile([P, T, 2], BF16, name=f"pairs_{s}_{u}", align_bytes=64)
+                cast_columns(pairs[:], x_raw[2 * s + u][:], T, X_SCALAR[2 * s + u])
+                window = pairs[:].rearrange("p w e -> p (w e)").bitcast(U32)
+                nc.vector.tensor_copy(out=picked[:, :, u], in_=window.indirect(offsets[:]))
+            scales = g_scales_0 if s == 0 else planes
+            nc.vector.quantize_mx(
+                out=g_codes[s][:].bitcast(FP8X4),
+                scales=scales[:],
+                in_=picked[:].rearrange("p n u -> p (n u)").bitcast(BF16),
+            )
 
-        def gather_codes(s):
-            nc.vector.tensor_copy(out=g_codes[s][:], in_=x_codes[s][:].indirect(offsets[:]))
-
-        quantize_atoms(0)
-        gather_codes(0)
-        quantize_atoms(1)
+        pick_atoms(0)
+        pick_atoms(1)
 
         def weights(raw, name, cut):
             codes = keep.tile([P, H], U32, name=f"{name}_codes", align_bytes=64)
@@ -98,15 +99,14 @@ def tile_picked_schnet_sigmoid_e_kernel(tc, xT, eT, w1, w3, w2, offs, out):
             dst = grouped[:].rearrange("p t m j -> p m j t")
             src = raw[:].rearrange("p j (m t) -> p m j t", t=PACK)
             nc.scalar.copy(out=dst[:, :cut], in_=src[:, :cut])
-            nc.vector.tensor_copy(out=dst[:, cut:], in_=src[:, cut:])
+            if cut < P:
+                nc.vector.tensor_copy(out=dst[:, cut:], in_=src[:, cut:])
             nc.vector.quantize_mx(
                 out=codes[:].bitcast(FP8X4), scales=scales[:], in_=grouped[:].rearrange("p t m j -> p (t m j)")
             )
             return codes, scales
 
         w1_q = [weights(w1_raw[0], "w1_0", W1_SCALAR[0])]
-        nc.vector.tensor_copy(out=g_scales[:], in_=x_scales[:].indirect(offsets[:]))
-        gather_codes(1)
         w1_q.append(weights(w1_raw[1], "w1_1", W1_SCALAR[1]))
         w3_codes, w3_scales = weights(w3_raw, "w3", W3_SCALAR)
 
@@ -114,7 +114,7 @@ def tile_picked_schnet_sigmoid_e_kernel(tc, xT, eT, w1, w3, w2, offs, out):
 
         def product_c(n):
             cols = slice(n * CHUNK, (n + 1) * CHUNK)
-            c_banks[n] = psum.tile([P, PACK, CHUNK], F32, name=f"c_{n}")
+            c_banks[n] = psum.tile([P, PACK, CHUNK], F32, name=f"c_{n}", tag=C_BANK[n])
             for t in range(PACK):
                 rows = slice(t * P, (t + 1) * P)
                 for s in range(2):
@@ -123,23 +123,24 @@ def tile_picked_schnet_sigmoid_e_kernel(tc, xT, eT, w1, w3, w2, offs, out):
                         lhsT=w1_q[s][0][:, rows].bitcast(FP8X4),
                         lhsT_scale=w1_q[s][1][:, rows],
                         rhs=g_codes[s][:, cols].bitcast(FP8X4),
-                        rhs_scale=g_scales[4 * s : P, cols],
+                        rhs_scale=(g_scales_0 if s == 0 else planes)[:, cols],
                         start=(s == 0),
                         stop=(s == 1),
                     )
 
         e_codes = [keep.tile([P, 256], U32, name=f"e_codes_{h}", align_bytes=64) for h in range(2)]
-        e_scales = [keep.tile([P, 256], U8, name=f"e_scales_{h}", align_bytes=64) for h in range(2)]
+        e_early = keep.tile([P, 256], U8, name="e_early", align_bytes=64)
+        e_scales = [e_early[:], planes[4:P, 256:]]
 
         def edges(h):
-            grouped = keep.tile([P, 256, PACK], BF16, name=f"e_grouped_{h}", align_bytes=64)
-            cast_columns(grouped[:], e_raw[h][:], 256, E_SCALAR[h])
             for q in range(2):
                 part = slice(q * CHUNK, (q + 1) * CHUNK)
+                grouped = keep.tile([P, CHUNK, PACK], BF16, name=f"e_grouped_{h}_{q}", align_bytes=64)
+                cast_columns(grouped[:], e_raw[h][:, :, part], CHUNK, E_SCALAR[2 * h + q])
                 nc.vector.quantize_mx(
                     out=e_codes[h][:, part].bitcast(FP8X4),
                     scales=e_scales[h][:, part],
-                    in_=grouped[:, part, :].rearrange("p w t -> p (w t)"),
+                    in_=grouped[:].rearrange("p w t -> p (w t)"),
                 )
 
         gates = {}
@@ -147,7 +148,7 @@ def tile_picked_schnet_sigmoid_e_kernel(tc, xT, eT, w1, w3, w2, offs, out):
         def gate(n):
             h, q = divmod(n, 2)
             part = slice(q * CHUNK, (q + 1) * CHUNK)
-            f_bank = ring.tile([P, PACK, CHUNK], F32, name="f_bank")
+            f_bank = psum.tile([P, PACK, CHUNK], F32, name=f"f_{n}", tag=F_BANK[n])
             for t in range(PACK):
                 rows = slice(t * P, (t + 1) * P)
                 nc.tensor.matmul_mx(
@@ -160,23 +161,16 @@ def tile_picked_schnet_sigmoid_e_kernel(tc, xT, eT, w1, w3, w2, offs, out):
                     stop=True,
                 )
             gates[n] = keep.tile([P, CHUNK, PACK], F32, name=f"gate_{n}", align_bytes=64)
-            for half in HALVES:
-                nc.scalar.activation(
-                    out=gates[n][:, half, :], in_=f_bank[:, :, half].rearrange("p t n -> p n t"), func=SIGMOID
-                )
+            nc.scalar.activation(out=gates[n][:], in_=f_bank[:].rearrange("p t n -> p n t"), func=SIGMOID)
 
         z_codes = {}
         z_scales = {}
 
         def message(n):
             z = keep.tile([P, CHUNK, PACK], BF16, name=f"z_{n}", align_bytes=64)
-            for half in HALVES:
-                nc.vector.tensor_tensor(
-                    out=z[:, half, :],
-                    in0=c_banks[n][:, :, half].rearrange("p t n -> p n t"),
-                    in1=gates[n][:, half, :],
-                    op=MULT,
-                )
+            nc.vector.tensor_tensor(
+                out=z[:], in0=c_banks[n][:].rearrange("p t n -> p n t"), in1=gates[n][:], op=MULT
+            )
             z_codes[n] = keep.tile([P, CHUNK], U32, name=f"z_codes_{n}", align_bytes=64)
             z_scales[n] = keep.tile([P, CHUNK], U8, name=f"z_scales_{n}", align_bytes=64)
             nc.vector.quantize_mx(
@@ -187,7 +181,7 @@ def tile_picked_schnet_sigmoid_e_kernel(tc, xT, eT, w1, w3, w2, offs, out):
         w2_scales = keep.tile([P, N], U8, name="w2_scales", align_bytes=64)
 
         def project(n):
-            o_bank = ring.tile([P, CHUNK], F32, name="o_bank")
+            o_bank = psum.tile([P, CHUNK], F32, name=f"o_{n}", tag=F_BANK[n])
             nc.tensor.matmul_mx(
                 out=o_bank[:],
                 lhsT=w2_codes[:].bitcast(FP8X4),
@@ -201,24 +195,23 @@ def tile_picked_schnet_sigmoid_e_kernel(tc, xT, eT, w1, w3, w2, offs, out):
             nc.scalar.copy(out=result[:], in_=o_bank[:])
             nc.sync.dma_start(out=out[:, n * CHUNK : (n + 1) * CHUNK], in_=result[:])
 
-        edges(0)
         product_c(0)
         product_c(1)
+        edges(0)
         gate(0)
         gate(1)
         edges(1)
+        gate(2)
+        gate(3)
+        product_c(2)
+        product_c(3)
         message(0)
         w2_grouped = keep.tile([P, N, PACK], BF16, name="w2_grouped", align_bytes=64)
         cast_columns(w2_grouped[:], w2_raw[:], N, W2_SCALAR)
         nc.vector.quantize_mx(
             out=w2_codes[:].bitcast(FP8X4), scales=w2_scales[:], in_=w2_grouped[:].rearrange("p w t -> p (w t)")
         )
-        gate(2)
-        product_c(2)
-        message(1)
-        gate(3)
-        product_c(3)
-        message(2)
-        message(3)
-        for n in range(4):
+        project(0)
+        for n in range(1, 4):
+            message(n)
             project(n)

@@ -5,6 +5,7 @@ import concourse.mybir as mybir
 F32 = mybir.dt.float32
 BF16 = mybir.dt.bfloat16
 U32 = mybir.dt.uint32
+I32 = mybir.dt.int32
 U16 = mybir.dt.uint16
 U8 = mybir.dt.uint8
 FP8X4 = mybir.dt.float8_e4m3fn_x4
@@ -76,12 +77,16 @@ def tile_picked_schnet_sigmoid_e_kernel(tc, xT, eT, w1, w3, w2, offs, out):
         planes = keep.tile([P, S], U8, name="planes", align_bytes=64)
 
         def pick_atoms(s):
+            halves = keep.tile([P, 2, S], U32, name=f"halves_{s}", align_bytes=64)
             picked = keep.tile([P, S, 2], U32, name=f"picked_{s}", align_bytes=64)
             for u in range(2):
                 pairs = keep.tile([P, T, 2], BF16, name=f"pairs_{s}_{u}", align_bytes=64)
                 cast_columns(pairs[:], x_raw[2 * s + u][:], T, X_SCALAR[2 * s + u])
                 window = pairs[:].rearrange("p w e -> p (w e)").bitcast(U32)
-                nc.vector.tensor_copy(out=picked[:, :, u], in_=window.indirect(offsets[:]))
+                nc.vector.tensor_copy(out=halves[:, u, :], in_=window.indirect(offsets[:]))
+            dst = picked[:].bitcast(I32).rearrange("p (c i) u -> p c u i", i=2)
+            src = halves[:].bitcast(I32).rearrange("p u (c i) -> p c u i", i=2)
+            nc.vector.tensor_copy(out=dst, in_=src)
             scales = g_scales_0 if s == 0 else planes
             nc.vector.quantize_mx(
                 out=g_codes[s][:].bitcast(FP8X4),

@@ -20,9 +20,15 @@ PACK = 4
 K_PASS = P * PACK
 CHUNK = 128
 
-X_SCALAR = (336, 400, 760, 680)
+X_SCALAR = (336, 360, 800, 680)
 W1_SCALAR = (128, 76)
-W3_SCALAR = 44
+W3_SCALAR = (44,)
+W3_PARTS = 1
+HOLDS = {2: 2, 3: 3}
+ORDER = "c0 c1 e0 g0 e1 g1 e2 e3 g2 g3 c2 c3 m0 w m1 p0 m2 p1 m3 p2 p3"
+W2_BEFORE = 4
+X_PARTS = 2
+E_LOADS = ((0, 2), (2, 2))
 E_SCALAR = (128, 128, 0, 128)
 W2_SCALAR = 0
 C_BANK = ("bank_0", "bank_1", "bank_2", "bank_3")
@@ -64,9 +70,19 @@ def tile_picked_schnet_sigmoid_e_kernel(tc, xT, eT, w1, w3, w2, offs, out):
         nc.sync.dma_start(offsets[:], offs)
         x_raw.extend([load_pair(0, 1), load_pair(1, 0), load_pair(1, 1)])
         w1_raw = [load(w1[s * K_PASS : (s + 1) * K_PASS, :], [P, PACK, H], f"w1_raw_{s}") for s in range(2)]
-        w3_raw = load(w3, [P, PACK, H], "w3_raw")
-        e_raw = [load(eT[:, h * 256 : (h + 1) * 256], [P, PACK, 256], f"e_raw_{h}") for h in range(2)]
-        w2_raw = load(w2, [P, PACK, N], "w2_raw")
+        w3_width = H // len(W3_SCALAR)
+        w3_raw = [
+            load(w3[:, h * w3_width : (h + 1) * w3_width], [P, PACK, w3_width], f"w3_raw_{h}")
+            for h in range(len(W3_SCALAR))
+        ]
+        e_raw = []
+        for first, count in E_LOADS:
+            if first == W2_BEFORE:
+                w2_raw = load(w2, [P, PACK, N], "w2_raw")
+            raw = load(eT[:, first * CHUNK : (first + count) * CHUNK], [P, PACK, count * CHUNK], f"e_raw_{first}")
+            e_raw.extend([raw[:, :, q * CHUNK : (q + 1) * CHUNK] for q in range(count)])
+        if W2_BEFORE == 4:
+            w2_raw = load(w2, [P, PACK, N], "w2_raw")
 
         warm = keep.tile([P, 1], F32, name="warm")
         nc.vector.memset(warm[:], 0.0)
@@ -79,20 +95,25 @@ def tile_picked_schnet_sigmoid_e_kernel(tc, xT, eT, w1, w3, w2, offs, out):
         def pick_atoms(s):
             halves = keep.tile([P, 2, S], U32, name=f"halves_{s}", align_bytes=64)
             picked = keep.tile([P, S, 2], U32, name=f"picked_{s}", align_bytes=64)
+            parts = [slice(q * S // X_PARTS, (q + 1) * S // X_PARTS) for q in range(X_PARTS)]
             for u in range(2):
                 pairs = keep.tile([P, T, 2], BF16, name=f"pairs_{s}_{u}", align_bytes=64)
                 cast_columns(pairs[:], x_raw[2 * s + u][:], T, X_SCALAR[2 * s + u])
                 window = pairs[:].rearrange("p w e -> p (w e)").bitcast(U32)
-                nc.vector.tensor_copy(out=halves[:, u, :], in_=window.indirect(offsets[:]))
-            dst = picked[:].bitcast(I32).rearrange("p (c i) u -> p c u i", i=2)
-            src = halves[:].bitcast(I32).rearrange("p u (c i) -> p c u i", i=2)
-            nc.vector.tensor_copy(out=dst, in_=src)
+                for part in parts if u == 1 else [slice(0, S)]:
+                    listed = offsets[:, part.start // 16 : part.stop // 16]
+                    nc.vector.tensor_copy(out=halves[:, u, part], in_=window.indirect(listed))
+            for part in parts:
+                dst = picked[:, part, :].bitcast(I32).rearrange("p (c i) u -> p c u i", i=2)
+                src = halves[:, :, part].bitcast(I32).rearrange("p u (c i) -> p c u i", i=2)
+                nc.vector.tensor_copy(out=dst, in_=src)
             scales = g_scales_0 if s == 0 else planes
-            nc.vector.quantize_mx(
-                out=g_codes[s][:].bitcast(FP8X4),
-                scales=scales[:],
-                in_=picked[:].rearrange("p n u -> p (n u)").bitcast(BF16),
-            )
+            for part in parts:
+                nc.vector.quantize_mx(
+                    out=g_codes[s][:, part].bitcast(FP8X4),
+                    scales=scales[:, part],
+                    in_=picked[:, part, :].rearrange("p n u -> p (n u)").bitcast(BF16),
+                )
 
         pick_atoms(0)
         pick_atoms(1)
@@ -113,7 +134,23 @@ def tile_picked_schnet_sigmoid_e_kernel(tc, xT, eT, w1, w3, w2, offs, out):
 
         w1_q = [weights(w1_raw[0], "w1_0", W1_SCALAR[0])]
         w1_q.append(weights(w1_raw[1], "w1_1", W1_SCALAR[1]))
-        w3_codes, w3_scales = weights(w3_raw, "w3", W3_SCALAR)
+        w3_codes = keep.tile([P, H], U32, name="w3_codes", align_bytes=64)
+        w3_scales = keep.tile([P, H], U8, name="w3_scales", align_bytes=64)
+        w3_grouped = keep.tile([P, PACK, P, PACK], BF16, name="w3_grouped", align_bytes=64)
+        for h in range(len(W3_SCALAR)):
+            dst = w3_grouped[:, :, h * w3_width // 4 : (h + 1) * w3_width // 4, :].rearrange("p t m j -> p m j t")
+            src = w3_raw[h][:].rearrange("p j (m t) -> p m j t", t=PACK)
+            cut = W3_SCALAR[h]
+            nc.scalar.copy(out=dst[:, :cut], in_=src[:, :cut])
+            if cut < w3_width // 4:
+                nc.vector.tensor_copy(out=dst[:, cut:], in_=src[:, cut:])
+        for u in range(W3_PARTS):
+            cols = slice(u * H // W3_PARTS, (u + 1) * H // W3_PARTS)
+            nc.vector.quantize_mx(
+                out=w3_codes[:, cols].bitcast(FP8X4),
+                scales=w3_scales[:, cols],
+                in_=w3_grouped[:, u * 4 // W3_PARTS : (u + 1) * 4 // W3_PARTS].rearrange("p t m j -> p (t m j)"),
+            )
 
         c_banks = {}
 
@@ -133,26 +170,25 @@ def tile_picked_schnet_sigmoid_e_kernel(tc, xT, eT, w1, w3, w2, offs, out):
                         stop=(s == 1),
                     )
 
-        e_codes = [keep.tile([P, 256], U32, name=f"e_codes_{h}", align_bytes=64) for h in range(2)]
-        e_early = keep.tile([P, 256], U8, name="e_early", align_bytes=64)
-        e_scales = [e_early[:], planes[4:P, 256:]]
+        e_codes = {}
+        e_scales = {}
 
-        def edges(h):
-            for q in range(2):
-                part = slice(q * CHUNK, (q + 1) * CHUNK)
-                grouped = keep.tile([P, CHUNK, PACK], BF16, name=f"e_grouped_{h}_{q}", align_bytes=64)
-                cast_columns(grouped[:], e_raw[h][:, :, part], CHUNK, E_SCALAR[2 * h + q])
-                nc.vector.quantize_mx(
-                    out=e_codes[h][:, part].bitcast(FP8X4),
-                    scales=e_scales[h][:, part],
-                    in_=grouped[:].rearrange("p w t -> p (w t)"),
-                )
+        def edges(n):
+            grouped = keep.tile([P, CHUNK, PACK], BF16, name=f"e_grouped_{n}", align_bytes=64)
+            cast_columns(grouped[:], e_raw[n], CHUNK, E_SCALAR[n])
+            e_codes[n] = keep.tile([P, CHUNK], U32, name=f"e_codes_{n}", align_bytes=64)
+            if n in HOLDS:
+                e_scales[n] = planes[4:P, HOLDS[n] * CHUNK : (HOLDS[n] + 1) * CHUNK]
+            else:
+                own = keep.tile([P, CHUNK], U8, name=f"e_scales_{n}", align_bytes=64)
+                e_scales[n] = own[:]
+            nc.vector.quantize_mx(
+                out=e_codes[n][:].bitcast(FP8X4), scales=e_scales[n], in_=grouped[:].rearrange("p w t -> p (w t)")
+            )
 
         gates = {}
 
         def gate(n):
-            h, q = divmod(n, 2)
-            part = slice(q * CHUNK, (q + 1) * CHUNK)
             f_bank = psum.tile([P, PACK, CHUNK], F32, name=f"f_{n}", tag=F_BANK[n])
             for t in range(PACK):
                 rows = slice(t * P, (t + 1) * P)
@@ -160,8 +196,8 @@ def tile_picked_schnet_sigmoid_e_kernel(tc, xT, eT, w1, w3, w2, offs, out):
                     out=f_bank[:, t, :],
                     lhsT=w3_codes[:, rows].bitcast(FP8X4),
                     lhsT_scale=w3_scales[:, rows],
-                    rhs=e_codes[h][:, part].bitcast(FP8X4),
-                    rhs_scale=e_scales[h][:, part],
+                    rhs=e_codes[n][:].bitcast(FP8X4),
+                    rhs_scale=e_scales[n],
                     start=True,
                     stop=True,
                 )
@@ -200,23 +236,13 @@ def tile_picked_schnet_sigmoid_e_kernel(tc, xT, eT, w1, w3, w2, offs, out):
             nc.scalar.copy(out=result[:], in_=o_bank[:])
             nc.sync.dma_start(out=out[:, n * CHUNK : (n + 1) * CHUNK], in_=result[:])
 
-        product_c(0)
-        product_c(1)
-        edges(0)
-        gate(0)
-        gate(1)
-        edges(1)
-        gate(2)
-        gate(3)
-        product_c(2)
-        product_c(3)
-        message(0)
-        w2_grouped = keep.tile([P, N, PACK], BF16, name="w2_grouped", align_bytes=64)
-        cast_columns(w2_grouped[:], w2_raw[:], N, W2_SCALAR)
-        nc.vector.quantize_mx(
-            out=w2_codes[:].bitcast(FP8X4), scales=w2_scales[:], in_=w2_grouped[:].rearrange("p w t -> p (w t)")
-        )
-        project(0)
-        for n in range(1, 4):
-            message(n)
-            project(n)
+        def quantize_w2(n):
+            w2_grouped = keep.tile([P, N, PACK], BF16, name="w2_grouped", align_bytes=64)
+            cast_columns(w2_grouped[:], w2_raw[:], N, W2_SCALAR)
+            nc.vector.quantize_mx(
+                out=w2_codes[:].bitcast(FP8X4), scales=w2_scales[:], in_=w2_grouped[:].rearrange("p w t -> p (w t)")
+            )
+
+        steps = {"c": product_c, "e": edges, "g": gate, "m": message, "p": project, "w": quantize_w2}
+        for step in ORDER.split():
+            steps[step[0]](int(step[1:] or 0))

@@ -22,15 +22,14 @@ CHUNK = 128
 
 X_SCALAR = (336, 360, 800, 680)
 W1_SCALAR = (128, 76)
-W3_SCALAR = (44,)
-W3_PARTS = 1
+W3_SCALAR = 44
 HOLDS = {2: 2, 3: 3}
-ORDER = "c0 c1 e0 g0 e1 g1 e2 e3 g2 g3 c2 c3 m0 w m1 p0 m2 p1 m3 p2 p3"
+ORDER = "c0 c1 a0 E0 b0 Q0 b1 g0 E1 Q1 g1 E2 E3 Q2 g2 Q3 g3 c2 c3 M0 M1 M2 Z0 Z1 M3 W V Z2 Z3 p0 p1 p2 p3"
 W2_BEFORE = 4
 X_PARTS = 2
-E_LOADS = ((0, 2), (2, 2))
-E_SCALAR = (128, 128, 0, 128)
-W2_SCALAR = 0
+E_LOADS = ((0, 1), (1, 1), (2, 1), (3, 1))
+E_SCALAR = (0, 128, 128, 0)
+W2_SCALAR = 128
 C_BANK = ("bank_0", "bank_1", "bank_2", "bank_3")
 F_BANK = ("bank_4", "bank_5", "bank_6", "bank_7")
 
@@ -70,11 +69,7 @@ def tile_picked_schnet_sigmoid_e_kernel(tc, xT, eT, w1, w3, w2, offs, out):
         nc.sync.dma_start(offsets[:], offs)
         x_raw.extend([load_pair(0, 1), load_pair(1, 0), load_pair(1, 1)])
         w1_raw = [load(w1[s * K_PASS : (s + 1) * K_PASS, :], [P, PACK, H], f"w1_raw_{s}") for s in range(2)]
-        w3_width = H // len(W3_SCALAR)
-        w3_raw = [
-            load(w3[:, h * w3_width : (h + 1) * w3_width], [P, PACK, w3_width], f"w3_raw_{h}")
-            for h in range(len(W3_SCALAR))
-        ]
+        w3_raw = load(w3, [P, PACK, H], "w3_raw")
         e_raw = []
         for first, count in E_LOADS:
             if first == W2_BEFORE:
@@ -137,19 +132,23 @@ def tile_picked_schnet_sigmoid_e_kernel(tc, xT, eT, w1, w3, w2, offs, out):
         w3_codes = keep.tile([P, H], U32, name="w3_codes", align_bytes=64)
         w3_scales = keep.tile([P, H], U8, name="w3_scales", align_bytes=64)
         w3_grouped = keep.tile([P, PACK, P, PACK], BF16, name="w3_grouped", align_bytes=64)
-        for h in range(len(W3_SCALAR)):
-            dst = w3_grouped[:, :, h * w3_width // 4 : (h + 1) * w3_width // 4, :].rearrange("p t m j -> p m j t")
-            src = w3_raw[h][:].rearrange("p j (m t) -> p m j t", t=PACK)
-            cut = W3_SCALAR[h]
-            nc.scalar.copy(out=dst[:, :cut], in_=src[:, :cut])
-            if cut < w3_width // 4:
+        slots = PACK // 2
+
+        def cast_w3(h):
+            dst = w3_grouped[:].rearrange("p t m j -> p m j t")
+            src = w3_raw[:].rearrange("p j (m t) -> p m j t", t=PACK)
+            cut = W3_SCALAR
+            if cut > 0:
+                nc.scalar.copy(out=dst[:, :cut], in_=src[:, :cut])
+            if cut < P:
                 nc.vector.tensor_copy(out=dst[:, cut:], in_=src[:, cut:])
-        for u in range(W3_PARTS):
-            cols = slice(u * H // W3_PARTS, (u + 1) * H // W3_PARTS)
+
+        def quantize_w3(h):
+            cols = slice(h * slots * P, (h + 1) * slots * P)
             nc.vector.quantize_mx(
                 out=w3_codes[:, cols].bitcast(FP8X4),
                 scales=w3_scales[:, cols],
-                in_=w3_grouped[:, u * 4 // W3_PARTS : (u + 1) * 4 // W3_PARTS].rearrange("p t m j -> p (t m j)"),
+                in_=w3_grouped[:, h * slots : (h + 1) * slots].rearrange("p t m j -> p (t m j)"),
             )
 
         c_banks = {}
@@ -173,9 +172,14 @@ def tile_picked_schnet_sigmoid_e_kernel(tc, xT, eT, w1, w3, w2, offs, out):
         e_codes = {}
         e_scales = {}
 
+        e_grouped = {}
+
+        def cast_edges(n):
+            e_grouped[n] = keep.tile([P, CHUNK, PACK], BF16, name=f"e_grouped_{n}", align_bytes=64)
+            cast_columns(e_grouped[n][:], e_raw[n], CHUNK, E_SCALAR[n])
+
         def edges(n):
-            grouped = keep.tile([P, CHUNK, PACK], BF16, name=f"e_grouped_{n}", align_bytes=64)
-            cast_columns(grouped[:], e_raw[n], CHUNK, E_SCALAR[n])
+            grouped = e_grouped[n]
             e_codes[n] = keep.tile([P, CHUNK], U32, name=f"e_codes_{n}", align_bytes=64)
             if n in HOLDS:
                 e_scales[n] = planes[4:P, HOLDS[n] * CHUNK : (HOLDS[n] + 1) * CHUNK]
@@ -207,11 +211,17 @@ def tile_picked_schnet_sigmoid_e_kernel(tc, xT, eT, w1, w3, w2, offs, out):
         z_codes = {}
         z_scales = {}
 
+        z_tiles = {}
+
         def message(n):
             z = keep.tile([P, CHUNK, PACK], BF16, name=f"z_{n}", align_bytes=64)
+            z_tiles[n] = z
             nc.vector.tensor_tensor(
                 out=z[:], in0=c_banks[n][:].rearrange("p t n -> p n t"), in1=gates[n][:], op=MULT
             )
+
+        def quantize_z(n):
+            z = z_tiles[n]
             z_codes[n] = keep.tile([P, CHUNK], U32, name=f"z_codes_{n}", align_bytes=64)
             z_scales[n] = keep.tile([P, CHUNK], U8, name=f"z_scales_{n}", align_bytes=64)
             nc.vector.quantize_mx(
@@ -236,13 +246,17 @@ def tile_picked_schnet_sigmoid_e_kernel(tc, xT, eT, w1, w3, w2, offs, out):
             nc.scalar.copy(out=result[:], in_=o_bank[:])
             nc.sync.dma_start(out=out[:, n * CHUNK : (n + 1) * CHUNK], in_=result[:])
 
-        def quantize_w2(n):
-            w2_grouped = keep.tile([P, N, PACK], BF16, name="w2_grouped", align_bytes=64)
+        w2_grouped = keep.tile([P, N, PACK], BF16, name="w2_grouped", align_bytes=64)
+
+        def cast_w2(n):
             cast_columns(w2_grouped[:], w2_raw[:], N, W2_SCALAR)
+
+        def quantize_w2(n):
             nc.vector.quantize_mx(
                 out=w2_codes[:].bitcast(FP8X4), scales=w2_scales[:], in_=w2_grouped[:].rearrange("p w t -> p (w t)")
             )
 
-        steps = {"c": product_c, "e": edges, "g": gate, "m": message, "p": project, "w": quantize_w2}
+        steps = {"c": product_c, "a": cast_w3, "b": quantize_w3, "E": cast_edges, "Q": edges, "g": gate}
+        steps.update({"M": message, "Z": quantize_z, "p": project, "W": cast_w2, "V": quantize_w2})
         for step in ORDER.split():
             steps[step[0]](int(step[1:] or 0))

@@ -20,8 +20,8 @@ PACK = 4
 K_PASS = P * PACK
 CHUNK = 128
 
-X_SCALAR = (336, 360, 800, 680)
-W1_SCALAR = (128, 76)
+X_SCALAR = (336, 360, 800, 720)
+W1_SCALAR = (12, 46)
 W3_SCALAR = 44
 HOLDS = {2: 2, 3: 3}
 ORDER = "c0 c1 a0 E0 b0 Q0 b1 g0 E1 Q1 g1 E2 E3 Q2 g2 Q3 g3 c2 c3 M0 M1 M2 Z0 Z1 M3 W V Z2 Z3 p0 p1 p2 p3"
@@ -68,7 +68,9 @@ def tile_picked_schnet_sigmoid_e_kernel(tc, xT, eT, w1, w3, w2, offs, out):
         x_raw = [load_pair(0, 0)]
         nc.sync.dma_start(offsets[:], offs)
         x_raw.extend([load_pair(0, 1), load_pair(1, 0), load_pair(1, 1)])
-        w1_raw = [load(w1[s * K_PASS : (s + 1) * K_PASS, :], [P, PACK, H], f"w1_raw_{s}") for s in range(2)]
+        w1_raw = keep.tile([P, 2, PACK, H], F32, name="w1_raw", align_bytes=64)
+        for s in range(2):
+            nc.sync.dma_start(out=w1_raw[:, s], in_=rows_of_4(w1[s * K_PASS : (s + 1) * K_PASS, :]))
         w3_raw = load(w3, [P, PACK, H], "w3_raw")
         e_raw = []
         for first, count in E_LOADS:
@@ -113,22 +115,22 @@ def tile_picked_schnet_sigmoid_e_kernel(tc, xT, eT, w1, w3, w2, offs, out):
         pick_atoms(0)
         pick_atoms(1)
 
-        def weights(raw, name, cut):
-            codes = keep.tile([P, H], U32, name=f"{name}_codes", align_bytes=64)
-            scales = keep.tile([P, H], U8, name=f"{name}_scales", align_bytes=64)
-            grouped = keep.tile([P, PACK, P, PACK], BF16, name=f"{name}_grouped", align_bytes=64)
-            dst = grouped[:].rearrange("p t m j -> p m j t")
-            src = raw[:].rearrange("p j (m t) -> p m j t", t=PACK)
-            nc.scalar.copy(out=dst[:, :cut], in_=src[:, :cut])
-            if cut < P:
-                nc.vector.tensor_copy(out=dst[:, cut:], in_=src[:, cut:])
+        w1_codes = keep.tile([P, 2, H], U32, name="w1_codes", align_bytes=64)
+        w1_scales = keep.tile([P, 2, H], U8, name="w1_scales", align_bytes=64)
+        w1_grouped = keep.tile([P, 2, PACK, P, PACK], BF16, name="w1_grouped", align_bytes=64)
+        dst = w1_grouped[:].rearrange("p s t m j -> p s m j t")
+        src = w1_raw[:].rearrange("p s j (m t) -> p s m j t", t=PACK)
+        both, alone = W1_SCALAR
+        nc.scalar.copy(out=dst[:, 0, both:], in_=src[:, 0, both:])
+        nc.vector.tensor_copy(out=dst[:, 1, both + alone :], in_=src[:, 1, both + alone :])
+        nc.scalar.copy(out=dst[:, :, :both], in_=src[:, :, :both])
+        nc.scalar.copy(out=dst[:, 1, both : both + alone], in_=src[:, 1, both : both + alone])
+        for s in range(2):
             nc.vector.quantize_mx(
-                out=codes[:].bitcast(FP8X4), scales=scales[:], in_=grouped[:].rearrange("p t m j -> p (t m j)")
+                out=w1_codes[:, s, :].bitcast(FP8X4),
+                scales=w1_scales[:, s, :],
+                in_=w1_grouped[:, s].rearrange("p t m j -> p (t m j)"),
             )
-            return codes, scales
-
-        w1_q = [weights(w1_raw[0], "w1_0", W1_SCALAR[0])]
-        w1_q.append(weights(w1_raw[1], "w1_1", W1_SCALAR[1]))
         w3_codes = keep.tile([P, H], U32, name="w3_codes", align_bytes=64)
         w3_scales = keep.tile([P, H], U8, name="w3_scales", align_bytes=64)
         w3_grouped = keep.tile([P, PACK, P, PACK], BF16, name="w3_grouped", align_bytes=64)
@@ -161,8 +163,8 @@ def tile_picked_schnet_sigmoid_e_kernel(tc, xT, eT, w1, w3, w2, offs, out):
                 for s in range(2):
                     nc.tensor.matmul_mx(
                         out=c_banks[n][:, t, :],
-                        lhsT=w1_q[s][0][:, rows].bitcast(FP8X4),
-                        lhsT_scale=w1_q[s][1][:, rows],
+                        lhsT=w1_codes[:, s, rows].bitcast(FP8X4),
+                        lhsT_scale=w1_scales[:, s, rows],
                         rhs=g_codes[s][:, cols].bitcast(FP8X4),
                         rhs_scale=(g_scales_0 if s == 0 else planes)[:, cols],
                         start=(s == 0),

@@ -23,8 +23,8 @@ CHUNK = 128
 X_SCALAR = (336, 360, 800, 720)
 W1_SCALAR = (12, 46)
 W3_SCALAR = 44
-HOLDS = {2: 2, 3: 3}
-ORDER = "c0 c1 a0 E0 b0 Q0 b1 g0 E1 Q1 g1 E2 E3 Q2 g2 Q3 g3 c2 c3 M0 M1 M2 Z0 Z1 M3 W V Z2 Z3 p0 p1 p2 p3"
+HOLDS = {3: 3}
+ORDER = "c0 c1 c2 a0 E0 b0 Q0 b1 g0 E1 Q1 g1 E2 E3 Q2 g2 Q3 g3 c3 M0 M1 M2 Z0 Z1 M3 W V Z2 Z3 p0 p1 p2 p3"
 W2_BEFORE = 4
 X_PARTS = 2
 E_LOADS = ((0, 1), (1, 1), (2, 1), (3, 1))
@@ -114,6 +114,18 @@ def tile_picked_schnet_sigmoid_e_kernel(tc, xT, eT, w1, w3, w2, offs, out):
 
         pick_atoms(0)
         pick_atoms(1)
+
+        idle_bank = psum.tile([P, 2, 2 * CHUNK], F32, name="idle_bank", tag=F_BANK[3])
+        for i in range(6):
+            nc.tensor.matmul_mx(
+                out=idle_bank[:, i % 2, :],
+                lhsT=g_codes[1][:, 2 * CHUNK : 3 * CHUNK].bitcast(FP8X4),
+                lhsT_scale=planes[:, 2 * CHUNK : 3 * CHUNK],
+                rhs=g_codes[1][:, 2 * CHUNK :].bitcast(FP8X4),
+                rhs_scale=planes[:, 2 * CHUNK :],
+                start=True,
+                stop=True,
+            )
 
         w1_codes = keep.tile([P, 2, H], U32, name="w1_codes", align_bytes=64)
         w1_scales = keep.tile([P, 2, H], U8, name="w1_scales", align_bytes=64)

@@ -27,8 +27,8 @@ HOLDS = {3: 3}
 ORDER = "c0 c1 c2 a0 E0 b0 Q0 b1 g0 E1 Q1 g1 E2 E3 Q2 g2 Q3 g3 c3 M0 M1 M2 Z0 Z1 M3 W V Z2 Z3 p0 p1 p2 p3"
 W2_BEFORE = 4
 X_PARTS = 2
-E_LOADS = ((0, 1), (1, 1), (2, 1), (3, 1))
-E_SCALAR = (0, 128, 128, 0)
+E_LOADS = ((0, 1), (1, 1), (2, 2))
+E_SCALAR = (0, 128, 0, 0)
 W2_SCALAR = 128
 C_BANK = ("bank_0", "bank_1", "bank_2", "bank_3")
 F_BANK = ("bank_4", "bank_5", "bank_6", "bank_7")

@@ -19,19 +19,15 @@ P = 128
 PACK = 4
 K_PASS = P * PACK
 CHUNK = 128
+CHUNKS = S // CHUNK
+LAST = CHUNKS - 1
 
-X_SCALAR = (336, 360, 800, 720)
-W1_SCALAR = (12, 46)
-W3_SCALAR = 44
-HOLDS = {3: 3}
-ORDER = "c0 c1 c2 a0 E0 b0 Q0 b1 g0 E1 Q1 g1 E2 E3 Q2 g2 Q3 g3 c3 M0 M1 M2 Z0 Z1 M3 W V Z2 Z3 p0 p1 p2 p3"
-W2_BEFORE = 4
-X_PARTS = 2
-E_LOADS = ((0, 1), (1, 1), (2, 2))
-E_SCALAR = (0, 128, 0, 0)
-W2_SCALAR = 128
-C_BANK = ("bank_0", "bank_1", "bank_2", "bank_3")
-F_BANK = ("bank_4", "bank_5", "bank_6", "bank_7")
+X_SCALAR_COLUMNS = (336, 360, 800, 720)
+W1_BOTH, W1_ALONE = 12, 46
+W3_SCALAR_ROWS = 44
+EDGE_LOADS = ((0, 1), (1, 1), (2, 2))
+SCALAR_EDGE_CHUNK = 1
+WARM_UP_PASSES = 5
 
 
 def tile_picked_schnet_sigmoid_e_kernel(tc, xT, eT, w1, w3, w2, offs, out):
@@ -40,7 +36,10 @@ def tile_picked_schnet_sigmoid_e_kernel(tc, xT, eT, w1, w3, w2, offs, out):
     def rows_of_4(dram):
         return dram.rearrange("(p j) w -> p j w", j=PACK)
 
-    def cast_columns(dst, src, width, scalar_width):
+    def chunk(n):
+        return slice(n * CHUNK, (n + 1) * CHUNK)
+
+    def round_columns(dst, src, width, scalar_width):
         dst = dst.rearrange("p (c i) t -> p c t i", i=4)
         src = src.rearrange("p t (c i) -> p c t i", i=4)
         cut = (width - scalar_width) // 4
@@ -49,228 +48,206 @@ def tile_picked_schnet_sigmoid_e_kernel(tc, xT, eT, w1, w3, w2, offs, out):
         if cut < width // 4:
             nc.scalar.copy(out=dst[:, cut:], in_=src[:, cut:])
 
-    def load(dram, shape, name):
-        raw = keep.tile(shape, F32, name=name, align_bytes=64)
-        nc.sync.dma_start(out=raw[:], in_=rows_of_4(dram))
-        return raw
+    def quantize(codes, scales, values):
+        nc.vector.quantize_mx(out=codes.bitcast(FP8X4), scales=scales, in_=values)
+
+    def mx_pass(bank, lhs_codes, lhs_scales, rhs_codes, rhs_scales, start=True, stop=True):
+        nc.tensor.matmul_mx(
+            out=bank,
+            lhsT=lhs_codes.bitcast(FP8X4),
+            lhsT_scale=lhs_scales,
+            rhs=rhs_codes.bitcast(FP8X4),
+            rhs_scale=rhs_scales,
+            start=start,
+            stop=stop,
+        )
 
     with ExitStack() as ctx:
         keep = ctx.enter_context(tc.tile_pool(name="keep", bufs=1))
         psum = ctx.enter_context(tc.psum_pool(name="psum", bufs=1))
 
-        offsets = keep.tile([P, S // 16], U16, name="offsets")
-        def load_pair(s, u):
+        def load(dram, shape, name):
+            raw = keep.tile(shape, F32, name=name, align_bytes=64)
+            nc.sync.dma_start(out=raw[:], in_=rows_of_4(dram))
+            return raw
+
+        def load_row_pair(s, u):
             raw = keep.tile([P, 2, T], F32, name=f"x_raw_{s}_{u}", align_bytes=64)
-            rows = xT[s * K_PASS : (s + 1) * K_PASS, :].rearrange("(p j) w -> p j w", j=PACK)
+            rows = rows_of_4(xT[s * K_PASS : (s + 1) * K_PASS, :])
             nc.sync.dma_start(out=raw[:], in_=rows[:, 2 * u : 2 * u + 2, :])
             return raw
 
-        x_raw = [load_pair(0, 0)]
+        offsets = keep.tile([P, S // 16], U16, name="offsets")
+        x_raw = [load_row_pair(0, 0)]
         nc.sync.dma_start(offsets[:], offs)
-        x_raw.extend([load_pair(0, 1), load_pair(1, 0), load_pair(1, 1)])
+        x_raw.extend([load_row_pair(0, 1), load_row_pair(1, 0), load_row_pair(1, 1)])
         w1_raw = keep.tile([P, 2, PACK, H], F32, name="w1_raw", align_bytes=64)
         for s in range(2):
             nc.sync.dma_start(out=w1_raw[:, s], in_=rows_of_4(w1[s * K_PASS : (s + 1) * K_PASS, :]))
         w3_raw = load(w3, [P, PACK, H], "w3_raw")
         e_raw = []
-        for first, count in E_LOADS:
-            if first == W2_BEFORE:
-                w2_raw = load(w2, [P, PACK, N], "w2_raw")
+        for first, count in EDGE_LOADS:
             raw = load(eT[:, first * CHUNK : (first + count) * CHUNK], [P, PACK, count * CHUNK], f"e_raw_{first}")
-            e_raw.extend([raw[:, :, q * CHUNK : (q + 1) * CHUNK] for q in range(count)])
-        if W2_BEFORE == 4:
-            w2_raw = load(w2, [P, PACK, N], "w2_raw")
+            e_raw.extend([raw[:, :, chunk(q)] for q in range(count)])
+        w2_raw = load(w2, [P, PACK, N], "w2_raw")
 
         warm = keep.tile([P, 1], F32, name="warm")
         nc.vector.memset(warm[:], 0.0)
         nc.scalar.activation(out=warm[:], in_=warm[:], func=SIGMOID)
 
-        g_codes = [keep.tile([P, S], U32, name=f"g_codes_{s}", align_bytes=64) for s in range(2)]
-        g_scales_0 = keep.tile([P, S], U8, name="g_scales_0", align_bytes=64)
-        planes = keep.tile([P, S], U8, name="planes", align_bytes=64)
+        x_codes = [keep.tile([P, S], U32, name=f"x_codes_{s}", align_bytes=64) for s in range(2)]
+        x_scales = [keep.tile([P, S], U8, name=f"x_scales_{s}", align_bytes=64) for s in range(2)]
 
         def pick_atoms(s):
-            halves = keep.tile([P, 2, S], U32, name=f"halves_{s}", align_bytes=64)
+            words = keep.tile([P, 2, S], U32, name=f"words_{s}", align_bytes=64)
             picked = keep.tile([P, S, 2], U32, name=f"picked_{s}", align_bytes=64)
-            parts = [slice(q * S // X_PARTS, (q + 1) * S // X_PARTS) for q in range(X_PARTS)]
+            halves = [slice(0, S // 2), slice(S // 2, S)]
             for u in range(2):
                 pairs = keep.tile([P, T, 2], BF16, name=f"pairs_{s}_{u}", align_bytes=64)
-                cast_columns(pairs[:], x_raw[2 * s + u][:], T, X_SCALAR[2 * s + u])
+                round_columns(pairs[:], x_raw[2 * s + u][:], T, X_SCALAR_COLUMNS[2 * s + u])
                 window = pairs[:].rearrange("p w e -> p (w e)").bitcast(U32)
-                for part in parts if u == 1 else [slice(0, S)]:
+                for part in halves if u == 1 else [slice(0, S)]:
                     listed = offsets[:, part.start // 16 : part.stop // 16]
-                    nc.vector.tensor_copy(out=halves[:, u, part], in_=window.indirect(listed))
-            for part in parts:
+                    nc.vector.tensor_copy(out=words[:, u, part], in_=window.indirect(listed))
+            for part in halves:
                 dst = picked[:, part, :].bitcast(I32).rearrange("p (c i) u -> p c u i", i=2)
-                src = halves[:, :, part].bitcast(I32).rearrange("p u (c i) -> p c u i", i=2)
+                src = words[:, :, part].bitcast(I32).rearrange("p u (c i) -> p c u i", i=2)
                 nc.vector.tensor_copy(out=dst, in_=src)
-            scales = g_scales_0 if s == 0 else planes
-            for part in parts:
-                nc.vector.quantize_mx(
-                    out=g_codes[s][:, part].bitcast(FP8X4),
-                    scales=scales[:, part],
-                    in_=picked[:, part, :].rearrange("p n u -> p (n u)").bitcast(BF16),
-                )
+            for part in halves:
+                values = picked[:, part, :].rearrange("p n u -> p (n u)").bitcast(BF16)
+                quantize(x_codes[s][:, part], x_scales[s][:, part], values)
 
         pick_atoms(0)
         pick_atoms(1)
 
-        idle_bank = psum.tile([P, 2, 2 * CHUNK], F32, name="idle_bank", tag=F_BANK[3])
-        for i in range(6):
-            nc.tensor.matmul_mx(
-                out=idle_bank[:, i % 2, :],
-                lhsT=g_codes[1][:, 2 * CHUNK : 3 * CHUNK].bitcast(FP8X4),
-                lhsT_scale=planes[:, 2 * CHUNK : 3 * CHUNK],
-                rhs=g_codes[1][:, 2 * CHUNK :].bitcast(FP8X4),
-                rhs_scale=planes[:, 2 * CHUNK :],
-                start=True,
-                stop=True,
+        def c_bank_tag(n):
+            return f"bank_{n}"
+
+        def f_bank_tag(n):
+            return f"bank_{CHUNKS + n}"
+
+        idle_bank = psum.tile([P, 2, 2 * CHUNK], F32, name="idle_bank", tag=f_bank_tag(LAST))
+        for i in range(WARM_UP_PASSES):
+            mx_pass(
+                idle_bank[:, i % 2, :],
+                x_codes[1][:, chunk(2)],
+                x_scales[1][:, chunk(2)],
+                x_codes[1][:, 2 * CHUNK :],
+                x_scales[1][:, 2 * CHUNK :],
             )
 
         w1_codes = keep.tile([P, 2, H], U32, name="w1_codes", align_bytes=64)
         w1_scales = keep.tile([P, 2, H], U8, name="w1_scales", align_bytes=64)
-        w1_grouped = keep.tile([P, 2, PACK, P, PACK], BF16, name="w1_grouped", align_bytes=64)
-        dst = w1_grouped[:].rearrange("p s t m j -> p s m j t")
+        w1_dealt = keep.tile([P, 2, PACK, P, PACK], BF16, name="w1_dealt", align_bytes=64)
+        dst = w1_dealt[:].rearrange("p s t m j -> p s m j t")
         src = w1_raw[:].rearrange("p s j (m t) -> p s m j t", t=PACK)
-        both, alone = W1_SCALAR
-        nc.scalar.copy(out=dst[:, 0, both:], in_=src[:, 0, both:])
-        nc.vector.tensor_copy(out=dst[:, 1, both + alone :], in_=src[:, 1, both + alone :])
-        nc.scalar.copy(out=dst[:, :, :both], in_=src[:, :, :both])
-        nc.scalar.copy(out=dst[:, 1, both : both + alone], in_=src[:, 1, both : both + alone])
+        cut = W1_BOTH + W1_ALONE
+        nc.scalar.copy(out=dst[:, 0, W1_BOTH:], in_=src[:, 0, W1_BOTH:])
+        nc.vector.tensor_copy(out=dst[:, 1, cut:], in_=src[:, 1, cut:])
+        nc.scalar.copy(out=dst[:, :, :W1_BOTH], in_=src[:, :, :W1_BOTH])
+        nc.scalar.copy(out=dst[:, 1, W1_BOTH:cut], in_=src[:, 1, W1_BOTH:cut])
         for s in range(2):
-            nc.vector.quantize_mx(
-                out=w1_codes[:, s, :].bitcast(FP8X4),
-                scales=w1_scales[:, s, :],
-                in_=w1_grouped[:, s].rearrange("p t m j -> p (t m j)"),
-            )
+            quantize(w1_codes[:, s, :], w1_scales[:, s, :], w1_dealt[:, s].rearrange("p t m j -> p (t m j)"))
+
         w3_codes = keep.tile([P, H], U32, name="w3_codes", align_bytes=64)
         w3_scales = keep.tile([P, H], U8, name="w3_scales", align_bytes=64)
-        w3_grouped = keep.tile([P, PACK, P, PACK], BF16, name="w3_grouped", align_bytes=64)
-        slots = PACK // 2
+        w3_dealt = keep.tile([P, PACK, P, PACK], BF16, name="w3_dealt", align_bytes=64)
+        w2_codes = keep.tile([P, N], U32, name="w2_codes", align_bytes=64)
+        w2_scales = keep.tile([P, N], U8, name="w2_scales", align_bytes=64)
+        w2_rounded = keep.tile([P, N, PACK], BF16, name="w2_rounded", align_bytes=64)
+        c_banks, e_rounded, e_codes, e_scales, gates, z_values, z_codes, z_scales = [{} for name in range(8)]
 
-        def cast_w3(h):
-            dst = w3_grouped[:].rearrange("p t m j -> p m j t")
-            src = w3_raw[:].rearrange("p j (m t) -> p m j t", t=PACK)
-            cut = W3_SCALAR
-            if cut > 0:
-                nc.scalar.copy(out=dst[:, :cut], in_=src[:, :cut])
-            if cut < P:
-                nc.vector.tensor_copy(out=dst[:, cut:], in_=src[:, cut:])
+        def slot(t):
+            return slice(t * P, (t + 1) * P)
+
+        def round_w3():
+            dealt = w3_dealt[:].rearrange("p t m j -> p m j t")
+            raw = w3_raw[:].rearrange("p j (m t) -> p m j t", t=PACK)
+            nc.scalar.copy(out=dealt[:, :W3_SCALAR_ROWS], in_=raw[:, :W3_SCALAR_ROWS])
+            nc.vector.tensor_copy(out=dealt[:, W3_SCALAR_ROWS:], in_=raw[:, W3_SCALAR_ROWS:])
 
         def quantize_w3(h):
-            cols = slice(h * slots * P, (h + 1) * slots * P)
-            nc.vector.quantize_mx(
-                out=w3_codes[:, cols].bitcast(FP8X4),
-                scales=w3_scales[:, cols],
-                in_=w3_grouped[:, h * slots : (h + 1) * slots].rearrange("p t m j -> p (t m j)"),
-            )
-
-        c_banks = {}
+            cols = slice(2 * h * P, 2 * (h + 1) * P)
+            values = w3_dealt[:, 2 * h : 2 * (h + 1)].rearrange("p t m j -> p (t m j)")
+            quantize(w3_codes[:, cols], w3_scales[:, cols], values)
 
         def product_c(n):
-            cols = slice(n * CHUNK, (n + 1) * CHUNK)
-            c_banks[n] = psum.tile([P, PACK, CHUNK], F32, name=f"c_{n}", tag=C_BANK[n])
+            c_banks[n] = psum.tile([P, PACK, CHUNK], F32, name=f"c_{n}", tag=c_bank_tag(n))
             for t in range(PACK):
-                rows = slice(t * P, (t + 1) * P)
                 for s in range(2):
-                    nc.tensor.matmul_mx(
-                        out=c_banks[n][:, t, :],
-                        lhsT=w1_codes[:, s, rows].bitcast(FP8X4),
-                        lhsT_scale=w1_scales[:, s, rows],
-                        rhs=g_codes[s][:, cols].bitcast(FP8X4),
-                        rhs_scale=(g_scales_0 if s == 0 else planes)[:, cols],
+                    mx_pass(
+                        c_banks[n][:, t, :],
+                        w1_codes[:, s, slot(t)],
+                        w1_scales[:, s, slot(t)],
+                        x_codes[s][:, chunk(n)],
+                        x_scales[s][:, chunk(n)],
                         start=(s == 0),
                         stop=(s == 1),
                     )
 
-        e_codes = {}
-        e_scales = {}
+        def round_edges(n):
+            e_rounded[n] = keep.tile([P, CHUNK, PACK], BF16, name=f"e_rounded_{n}", align_bytes=64)
+            round_columns(e_rounded[n][:], e_raw[n], CHUNK, CHUNK if n == SCALAR_EDGE_CHUNK else 0)
 
-        e_grouped = {}
-
-        def cast_edges(n):
-            e_grouped[n] = keep.tile([P, CHUNK, PACK], BF16, name=f"e_grouped_{n}", align_bytes=64)
-            cast_columns(e_grouped[n][:], e_raw[n], CHUNK, E_SCALAR[n])
-
-        def edges(n):
-            grouped = e_grouped[n]
+        def quantize_edges(n):
             e_codes[n] = keep.tile([P, CHUNK], U32, name=f"e_codes_{n}", align_bytes=64)
-            if n in HOLDS:
-                e_scales[n] = planes[4:P, HOLDS[n] * CHUNK : (HOLDS[n] + 1) * CHUNK]
+            if n == LAST:
+                e_scales[n] = x_scales[1][4:P, chunk(n)]
             else:
                 own = keep.tile([P, CHUNK], U8, name=f"e_scales_{n}", align_bytes=64)
                 e_scales[n] = own[:]
-            nc.vector.quantize_mx(
-                out=e_codes[n][:].bitcast(FP8X4), scales=e_scales[n], in_=grouped[:].rearrange("p w t -> p (w t)")
-            )
-
-        gates = {}
+            quantize(e_codes[n][:], e_scales[n], e_rounded[n][:].rearrange("p w t -> p (w t)"))
 
         def gate(n):
-            f_bank = psum.tile([P, PACK, CHUNK], F32, name=f"f_{n}", tag=F_BANK[n])
+            f_bank = psum.tile([P, PACK, CHUNK], F32, name=f"f_{n}", tag=f_bank_tag(n))
             for t in range(PACK):
-                rows = slice(t * P, (t + 1) * P)
-                nc.tensor.matmul_mx(
-                    out=f_bank[:, t, :],
-                    lhsT=w3_codes[:, rows].bitcast(FP8X4),
-                    lhsT_scale=w3_scales[:, rows],
-                    rhs=e_codes[n][:].bitcast(FP8X4),
-                    rhs_scale=e_scales[n],
-                    start=True,
-                    stop=True,
-                )
+                mx_pass(f_bank[:, t, :], w3_codes[:, slot(t)], w3_scales[:, slot(t)], e_codes[n][:], e_scales[n])
             gates[n] = keep.tile([P, CHUNK, PACK], F32, name=f"gate_{n}", align_bytes=64)
             nc.scalar.activation(out=gates[n][:], in_=f_bank[:].rearrange("p t n -> p n t"), func=SIGMOID)
 
-        z_codes = {}
-        z_scales = {}
-
-        z_tiles = {}
-
         def message(n):
-            z = keep.tile([P, CHUNK, PACK], BF16, name=f"z_{n}", align_bytes=64)
-            z_tiles[n] = z
-            nc.vector.tensor_tensor(
-                out=z[:], in0=c_banks[n][:].rearrange("p t n -> p n t"), in1=gates[n][:], op=MULT
-            )
+            z_values[n] = keep.tile([P, CHUNK, PACK], BF16, name=f"z_{n}", align_bytes=64)
+            c = c_banks[n][:].rearrange("p t n -> p n t")
+            nc.vector.tensor_tensor(out=z_values[n][:], in0=c, in1=gates[n][:], op=MULT)
 
         def quantize_z(n):
-            z = z_tiles[n]
             z_codes[n] = keep.tile([P, CHUNK], U32, name=f"z_codes_{n}", align_bytes=64)
             z_scales[n] = keep.tile([P, CHUNK], U8, name=f"z_scales_{n}", align_bytes=64)
-            nc.vector.quantize_mx(
-                out=z_codes[n][:].bitcast(FP8X4), scales=z_scales[n][:], in_=z[:].rearrange("p n t -> p (n t)")
-            )
-
-        w2_codes = keep.tile([P, N], U32, name="w2_codes", align_bytes=64)
-        w2_scales = keep.tile([P, N], U8, name="w2_scales", align_bytes=64)
+            quantize(z_codes[n][:], z_scales[n][:], z_values[n][:].rearrange("p n t -> p (n t)"))
 
         def project(n):
-            o_bank = psum.tile([P, CHUNK], F32, name=f"o_{n}", tag=F_BANK[n])
-            nc.tensor.matmul_mx(
-                out=o_bank[:],
-                lhsT=w2_codes[:].bitcast(FP8X4),
-                lhsT_scale=w2_scales[:],
-                rhs=z_codes[n][:].bitcast(FP8X4),
-                rhs_scale=z_scales[n][:],
-                start=True,
-                stop=True,
-            )
+            o_bank = psum.tile([P, CHUNK], F32, name=f"o_{n}", tag=f_bank_tag(n))
+            mx_pass(o_bank[:], w2_codes[:], w2_scales[:], z_codes[n][:], z_scales[n][:])
             result = keep.tile([P, CHUNK], F32, name=f"result_{n}")
             nc.scalar.copy(out=result[:], in_=o_bank[:])
-            nc.sync.dma_start(out=out[:, n * CHUNK : (n + 1) * CHUNK], in_=result[:])
+            nc.sync.dma_start(out=out[:, chunk(n)], in_=result[:])
 
-        w2_grouped = keep.tile([P, N, PACK], BF16, name="w2_grouped", align_bytes=64)
+        for n in range(LAST):
+            product_c(n)
 
-        def cast_w2(n):
-            cast_columns(w2_grouped[:], w2_raw[:], N, W2_SCALAR)
+        round_w3()
+        round_edges(0)
+        quantize_w3(0)
+        quantize_edges(0)
+        quantize_w3(1)
+        gate(0)
 
-        def quantize_w2(n):
-            nc.vector.quantize_mx(
-                out=w2_codes[:].bitcast(FP8X4), scales=w2_scales[:], in_=w2_grouped[:].rearrange("p w t -> p (w t)")
-            )
+        for first, count in EDGE_LOADS[1:]:
+            for n in range(first, first + count):
+                round_edges(n)
+            for n in range(first, first + count):
+                quantize_edges(n)
+                gate(n)
+        product_c(LAST)
 
-        steps = {"c": product_c, "a": cast_w3, "b": quantize_w3, "E": cast_edges, "Q": edges, "g": gate}
-        steps.update({"M": message, "Z": quantize_z, "p": project, "W": cast_w2, "V": quantize_w2})
-        for step in ORDER.split():
-            steps[step[0]](int(step[1:] or 0))
+        for n in range(LAST):
+            message(n)
+        quantize_z(0)
+        quantize_z(1)
+        message(LAST)
+        round_columns(w2_rounded[:], w2_raw[:], N, N)
+        quantize(w2_codes[:], w2_scales[:], w2_rounded[:].rearrange("p w t -> p (w t)"))
+        quantize_z(2)
+        quantize_z(LAST)
+        for n in range(CHUNKS):
+            project(n)

@@ -19,15 +19,19 @@ P = 128
 PACK = 4
 K_PASS = P * PACK
 CHUNK = 128
-CHUNKS = S // CHUNK
-LAST = CHUNKS - 1
 
-X_SCALAR_COLUMNS = (336, 360, 800, 720)
-W1_BOTH, W1_ALONE = 12, 46
-W3_SCALAR_ROWS = 44
-EDGE_LOADS = ((0, 1), (1, 1), (2, 2))
-SCALAR_EDGE_CHUNK = 1
-WARM_UP_PASSES = 5
+X_SCALAR = (336, 360, 800, 720)
+W1_SCALAR = (12, 46)
+W3_SCALAR = 44
+HOLDS = {3: 3}
+ORDER = "c0 c1 c2 a0 E0 b0 Q0 b1 g0 E1 Q1 g1 E2 E3 Q2 g2 Q3 g3 c3 M0 M1 M2 Z0 Z1 M3 W V Z2 Z3 p0 p1 p2 p3"
+W2_BEFORE = 4
+X_PARTS = 4
+E_LOADS = ((0, 1), (1, 1), (2, 2))
+E_SCALAR = (0, 128, 0, 0)
+W2_SCALAR = 128
+C_BANK = ("bank_0", "bank_1", "bank_2", "bank_3")
+F_BANK = ("bank_4", "bank_5", "bank_6", "bank_7")
 
 
 def tile_picked_schnet_sigmoid_e_kernel(tc, xT, eT, w1, w3, w2, offs, out):
@@ -36,10 +40,7 @@ def tile_picked_schnet_sigmoid_e_kernel(tc, xT, eT, w1, w3, w2, offs, out):
     def rows_of_4(dram):
         return dram.rearrange("(p j) w -> p j w", j=PACK)
 
-    def chunk(n):
-        return slice(n * CHUNK, (n + 1) * CHUNK)
-
-    def round_columns(dst, src, width, scalar_width):
+    def cast_columns(dst, src, width, scalar_width):
         dst = dst.rearrange("p (c i) t -> p c t i", i=4)
         src = src.rearrange("p t (c i) -> p c t i", i=4)
         cut = (width - scalar_width) // 4
@@ -48,206 +49,228 @@ def tile_picked_schnet_sigmoid_e_kernel(tc, xT, eT, w1, w3, w2, offs, out):
         if cut < width // 4:
             nc.scalar.copy(out=dst[:, cut:], in_=src[:, cut:])
 
-    def quantize(codes, scales, values):
-        nc.vector.quantize_mx(out=codes.bitcast(FP8X4), scales=scales, in_=values)
-
-    def mx_pass(bank, lhs_codes, lhs_scales, rhs_codes, rhs_scales, start=True, stop=True):
-        nc.tensor.matmul_mx(
-            out=bank,
-            lhsT=lhs_codes.bitcast(FP8X4),
-            lhsT_scale=lhs_scales,
-            rhs=rhs_codes.bitcast(FP8X4),
-            rhs_scale=rhs_scales,
-            start=start,
-            stop=stop,
-        )
+    def load(dram, shape, name):
+        raw = keep.tile(shape, F32, name=name, align_bytes=64)
+        nc.sync.dma_start(out=raw[:], in_=rows_of_4(dram))
+        return raw
 
     with ExitStack() as ctx:
         keep = ctx.enter_context(tc.tile_pool(name="keep", bufs=1))
         psum = ctx.enter_context(tc.psum_pool(name="psum", bufs=1))
 
-        def load(dram, shape, name):
-            raw = keep.tile(shape, F32, name=name, align_bytes=64)
-            nc.sync.dma_start(out=raw[:], in_=rows_of_4(dram))
-            return raw
-
-        def load_row_pair(s, u):
+        offsets = keep.tile([P, S // 16], U16, name="offsets")
+        def load_pair(s, u):
             raw = keep.tile([P, 2, T], F32, name=f"x_raw_{s}_{u}", align_bytes=64)
-            rows = rows_of_4(xT[s * K_PASS : (s + 1) * K_PASS, :])
+            rows = xT[s * K_PASS : (s + 1) * K_PASS, :].rearrange("(p j) w -> p j w", j=PACK)
             nc.sync.dma_start(out=raw[:], in_=rows[:, 2 * u : 2 * u + 2, :])
             return raw
 
-        offsets = keep.tile([P, S // 16], U16, name="offsets")
-        x_raw = [load_row_pair(0, 0)]
+        x_raw = [load_pair(0, 0)]
         nc.sync.dma_start(offsets[:], offs)
-        x_raw.extend([load_row_pair(0, 1), load_row_pair(1, 0), load_row_pair(1, 1)])
+        x_raw.extend([load_pair(0, 1), load_pair(1, 0), load_pair(1, 1)])
         w1_raw = keep.tile([P, 2, PACK, H], F32, name="w1_raw", align_bytes=64)
         for s in range(2):
             nc.sync.dma_start(out=w1_raw[:, s], in_=rows_of_4(w1[s * K_PASS : (s + 1) * K_PASS, :]))
         w3_raw = load(w3, [P, PACK, H], "w3_raw")
         e_raw = []
-        for first, count in EDGE_LOADS:
+        for first, count in E_LOADS:
+            if first == W2_BEFORE:
+                w2_raw = load(w2, [P, PACK, N], "w2_raw")
             raw = load(eT[:, first * CHUNK : (first + count) * CHUNK], [P, PACK, count * CHUNK], f"e_raw_{first}")
-            e_raw.extend([raw[:, :, chunk(q)] for q in range(count)])
-        w2_raw = load(w2, [P, PACK, N], "w2_raw")
+            e_raw.extend([raw[:, :, q * CHUNK : (q + 1) * CHUNK] for q in range(count)])
+        if W2_BEFORE == 4:
+            w2_raw = load(w2, [P, PACK, N], "w2_raw")
 
         warm = keep.tile([P, 1], F32, name="warm")
         nc.vector.memset(warm[:], 0.0)
         nc.scalar.activation(out=warm[:], in_=warm[:], func=SIGMOID)
 
-        x_codes = [keep.tile([P, S], U32, name=f"x_codes_{s}", align_bytes=64) for s in range(2)]
-        x_scales = [keep.tile([P, S], U8, name=f"x_scales_{s}", align_bytes=64) for s in range(2)]
+        g_codes = [keep.tile([P, S], U32, name=f"g_codes_{s}", align_bytes=64) for s in range(2)]
+        g_scales_0 = keep.tile([P, S], U8, name="g_scales_0", align_bytes=64)
+        planes = keep.tile([P, S], U8, name="planes", align_bytes=64)
 
         def pick_atoms(s):
-            words = keep.tile([P, 2, S], U32, name=f"words_{s}", align_bytes=64)
+            halves = keep.tile([P, 2, S], U32, name=f"halves_{s}", align_bytes=64)
             picked = keep.tile([P, S, 2], U32, name=f"picked_{s}", align_bytes=64)
-            halves = [slice(0, S // 2), slice(S // 2, S)]
+            parts = [slice(q * S // X_PARTS, (q + 1) * S // X_PARTS) for q in range(X_PARTS)]
             for u in range(2):
                 pairs = keep.tile([P, T, 2], BF16, name=f"pairs_{s}_{u}", align_bytes=64)
-                round_columns(pairs[:], x_raw[2 * s + u][:], T, X_SCALAR_COLUMNS[2 * s + u])
+                cast_columns(pairs[:], x_raw[2 * s + u][:], T, X_SCALAR[2 * s + u])
                 window = pairs[:].rearrange("p w e -> p (w e)").bitcast(U32)
-                for part in halves if u == 1 else [slice(0, S)]:
+                for part in parts:
                     listed = offsets[:, part.start // 16 : part.stop // 16]
-                    nc.vector.tensor_copy(out=words[:, u, part], in_=window.indirect(listed))
-            for part in halves:
+                    nc.vector.tensor_copy(out=halves[:, u, part], in_=window.indirect(listed))
+            for part in parts:
                 dst = picked[:, part, :].bitcast(I32).rearrange("p (c i) u -> p c u i", i=2)
-                src = words[:, :, part].bitcast(I32).rearrange("p u (c i) -> p c u i", i=2)
+                src = halves[:, :, part].bitcast(I32).rearrange("p u (c i) -> p c u i", i=2)
                 nc.vector.tensor_copy(out=dst, in_=src)
-            for part in halves:
-                values = picked[:, part, :].rearrange("p n u -> p (n u)").bitcast(BF16)
-                quantize(x_codes[s][:, part], x_scales[s][:, part], values)
+            scales = g_scales_0 if s == 0 else planes
+            for part in parts:
+                nc.vector.quantize_mx(
+                    out=g_codes[s][:, part].bitcast(FP8X4),
+                    scales=scales[:, part],
+                    in_=picked[:, part, :].rearrange("p n u -> p (n u)").bitcast(BF16),
+                )
 
         pick_atoms(0)
         pick_atoms(1)
 
-        def c_bank_tag(n):
-            return f"bank_{n}"
-
-        def f_bank_tag(n):
-            return f"bank_{CHUNKS + n}"
-
-        idle_bank = psum.tile([P, 2, 2 * CHUNK], F32, name="idle_bank", tag=f_bank_tag(LAST))
-        for i in range(WARM_UP_PASSES):
-            mx_pass(
-                idle_bank[:, i % 2, :],
-                x_codes[1][:, chunk(2)],
-                x_scales[1][:, chunk(2)],
-                x_codes[1][:, 2 * CHUNK :],
-                x_scales[1][:, 2 * CHUNK :],
+        idle_bank = psum.tile([P, 2, 2 * CHUNK], F32, name="idle_bank", tag=F_BANK[3])
+        for i in range(5):
+            nc.tensor.matmul_mx(
+                out=idle_bank[:, i % 2, :],
+                lhsT=g_codes[1][:, 2 * CHUNK : 3 * CHUNK].bitcast(FP8X4),
+                lhsT_scale=planes[:, 2 * CHUNK : 3 * CHUNK],
+                rhs=g_codes[1][:, 2 * CHUNK :].bitcast(FP8X4),
+                rhs_scale=planes[:, 2 * CHUNK :],
+                start=True,
+                stop=True,
             )
 
         w1_codes = keep.tile([P, 2, H], U32, name="w1_codes", align_bytes=64)
         w1_scales = keep.tile([P, 2, H], U8, name="w1_scales", align_bytes=64)
-        w1_dealt = keep.tile([P, 2, PACK, P, PACK], BF16, name="w1_dealt", align_bytes=64)
-        dst = w1_dealt[:].rearrange("p s t m j -> p s m j t")
+        w1_grouped = keep.tile([P, 2, PACK, P, PACK], BF16, name="w1_grouped", align_bytes=64)
+        dst = w1_grouped[:].rearrange("p s t m j -> p s m j t")
         src = w1_raw[:].rearrange("p s j (m t) -> p s m j t", t=PACK)
-        cut = W1_BOTH + W1_ALONE
-        nc.scalar.copy(out=dst[:, 0, W1_BOTH:], in_=src[:, 0, W1_BOTH:])
-        nc.vector.tensor_copy(out=dst[:, 1, cut:], in_=src[:, 1, cut:])
-        nc.scalar.copy(out=dst[:, :, :W1_BOTH], in_=src[:, :, :W1_BOTH])
-        nc.scalar.copy(out=dst[:, 1, W1_BOTH:cut], in_=src[:, 1, W1_BOTH:cut])
+        both, alone = W1_SCALAR
+        nc.scalar.copy(out=dst[:, 0, both:], in_=src[:, 0, both:])
+        nc.vector.tensor_copy(out=dst[:, 1, both + alone :], in_=src[:, 1, both + alone :])
+        nc.scalar.copy(out=dst[:, :, :both], in_=src[:, :, :both])
+        nc.scalar.copy(out=dst[:, 1, both : both + alone], in_=src[:, 1, both : both + alone])
         for s in range(2):
-            quantize(w1_codes[:, s, :], w1_scales[:, s, :], w1_dealt[:, s].rearrange("p t m j -> p (t m j)"))
-
+            nc.vector.quantize_mx(
+                out=w1_codes[:, s, :].bitcast(FP8X4),
+                scales=w1_scales[:, s, :],
+                in_=w1_grouped[:, s].rearrange("p t m j -> p (t m j)"),
+            )
         w3_codes = keep.tile([P, H], U32, name="w3_codes", align_bytes=64)
         w3_scales = keep.tile([P, H], U8, name="w3_scales", align_bytes=64)
-        w3_dealt = keep.tile([P, PACK, P, PACK], BF16, name="w3_dealt", align_bytes=64)
-        w2_codes = keep.tile([P, N], U32, name="w2_codes", align_bytes=64)
-        w2_scales = keep.tile([P, N], U8, name="w2_scales", align_bytes=64)
-        w2_rounded = keep.tile([P, N, PACK], BF16, name="w2_rounded", align_bytes=64)
-        c_banks, e_rounded, e_codes, e_scales, gates, z_values, z_codes, z_scales = [{} for name in range(8)]
+        w3_grouped = keep.tile([P, PACK, P, PACK], BF16, name="w3_grouped", align_bytes=64)
+        slots = PACK // 2
 
-        def slot(t):
-            return slice(t * P, (t + 1) * P)
-
-        def round_w3():
-            dealt = w3_dealt[:].rearrange("p t m j -> p m j t")
-            raw = w3_raw[:].rearrange("p j (m t) -> p m j t", t=PACK)
-            nc.scalar.copy(out=dealt[:, :W3_SCALAR_ROWS], in_=raw[:, :W3_SCALAR_ROWS])
-            nc.vector.tensor_copy(out=dealt[:, W3_SCALAR_ROWS:], in_=raw[:, W3_SCALAR_ROWS:])
+        def cast_w3(h):
+            dst = w3_grouped[:].rearrange("p t m j -> p m j t")
+            src = w3_raw[:].rearrange("p j (m t) -> p m j t", t=PACK)
+            cut = W3_SCALAR
+            if cut > 0:
+                nc.scalar.copy(out=dst[:, :cut], in_=src[:, :cut])
+            if cut < P:
+                nc.vector.tensor_copy(out=dst[:, cut:], in_=src[:, cut:])
 
         def quantize_w3(h):
-            cols = slice(2 * h * P, 2 * (h + 1) * P)
-            values = w3_dealt[:, 2 * h : 2 * (h + 1)].rearrange("p t m j -> p (t m j)")
-            quantize(w3_codes[:, cols], w3_scales[:, cols], values)
+            cols = slice(h * slots * P, (h + 1) * slots * P)
+            nc.vector.quantize_mx(
+                out=w3_codes[:, cols].bitcast(FP8X4),
+                scales=w3_scales[:, cols],
+                in_=w3_grouped[:, h * slots : (h + 1) * slots].rearrange("p t m j -> p (t m j)"),
+            )
+
+        c_banks = {}
 
         def product_c(n):
-            c_banks[n] = psum.tile([P, PACK, CHUNK], F32, name=f"c_{n}", tag=c_bank_tag(n))
+            cols = slice(n * CHUNK, (n + 1) * CHUNK)
+            c_banks[n] = psum.tile([P, PACK, CHUNK], F32, name=f"c_{n}", tag=C_BANK[n])
             for t in range(PACK):
+                rows = slice(t * P, (t + 1) * P)
                 for s in range(2):
-                    mx_pass(
-                        c_banks[n][:, t, :],
-                        w1_codes[:, s, slot(t)],
-                        w1_scales[:, s, slot(t)],
-                        x_codes[s][:, chunk(n)],
-                        x_scales[s][:, chunk(n)],
+                    nc.tensor.matmul_mx(
+                        out=c_banks[n][:, t, :],
+                        lhsT=w1_codes[:, s, rows].bitcast(FP8X4),
+                        lhsT_scale=w1_scales[:, s, rows],
+                        rhs=g_codes[s][:, cols].bitcast(FP8X4),
+                        rhs_scale=(g_scales_0 if s == 0 else planes)[:, cols],
                         start=(s == 0),
                         stop=(s == 1),
                     )
 
-        def round_edges(n):
-            e_rounded[n] = keep.tile([P, CHUNK, PACK], BF16, name=f"e_rounded_{n}", align_bytes=64)
-            round_columns(e_rounded[n][:], e_raw[n], CHUNK, CHUNK if n == SCALAR_EDGE_CHUNK else 0)
+        e_codes = {}
+        e_scales = {}
 
-        def quantize_edges(n):
+        e_grouped = {}
+
+        def cast_edges(n):
+            e_grouped[n] = keep.tile([P, CHUNK, PACK], BF16, name=f"e_grouped_{n}", align_bytes=64)
+            cast_columns(e_grouped[n][:], e_raw[n], CHUNK, E_SCALAR[n])
+
+        def edges(n):
+            grouped = e_grouped[n]
             e_codes[n] = keep.tile([P, CHUNK], U32, name=f"e_codes_{n}", align_bytes=64)
-            if n == LAST:
-                e_scales[n] = x_scales[1][4:P, chunk(n)]
+            if n in HOLDS:
+                e_scales[n] = planes[4:P, HOLDS[n] * CHUNK : (HOLDS[n] + 1) * CHUNK]
             else:
                 own = keep.tile([P, CHUNK], U8, name=f"e_scales_{n}", align_bytes=64)
                 e_scales[n] = own[:]
-            quantize(e_codes[n][:], e_scales[n], e_rounded[n][:].rearrange("p w t -> p (w t)"))
+            nc.vector.quantize_mx(
+                out=e_codes[n][:].bitcast(FP8X4), scales=e_scales[n], in_=grouped[:].rearrange("p w t -> p (w t)")
+            )
+
+        gates = {}
 
         def gate(n):
-            f_bank = psum.tile([P, PACK, CHUNK], F32, name=f"f_{n}", tag=f_bank_tag(n))
+            f_bank = psum.tile([P, PACK, CHUNK], F32, name=f"f_{n}", tag=F_BANK[n])
             for t in range(PACK):
-                mx_pass(f_bank[:, t, :], w3_codes[:, slot(t)], w3_scales[:, slot(t)], e_codes[n][:], e_scales[n])
+                rows = slice(t * P, (t + 1) * P)
+                nc.tensor.matmul_mx(
+                    out=f_bank[:, t, :],
+                    lhsT=w3_codes[:, rows].bitcast(FP8X4),
+                    lhsT_scale=w3_scales[:, rows],
+                    rhs=e_codes[n][:].bitcast(FP8X4),
+                    rhs_scale=e_scales[n],
+                    start=True,
+                    stop=True,
+                )
             gates[n] = keep.tile([P, CHUNK, PACK], F32, name=f"gate_{n}", align_bytes=64)
             nc.scalar.activation(out=gates[n][:], in_=f_bank[:].rearrange("p t n -> p n t"), func=SIGMOID)
 
+        z_codes = {}
+        z_scales = {}
+
+        z_tiles = {}
+
         def message(n):
-            z_values[n] = keep.tile([P, CHUNK, PACK], BF16, name=f"z_{n}", align_bytes=64)
-            c = c_banks[n][:].rearrange("p t n -> p n t")
-            nc.vector.tensor_tensor(out=z_values[n][:], in0=c, in1=gates[n][:], op=MULT)
+            z = keep.tile([P, CHUNK, PACK], BF16, name=f"z_{n}", align_bytes=64)
+            z_tiles[n] = z
+            nc.vector.tensor_tensor(
+                out=z[:], in0=c_banks[n][:].rearrange("p t n -> p n t"), in1=gates[n][:], op=MULT
+            )
 
         def quantize_z(n):
+            z = z_tiles[n]
             z_codes[n] = keep.tile([P, CHUNK], U32, name=f"z_codes_{n}", align_bytes=64)
             z_scales[n] = keep.tile([P, CHUNK], U8, name=f"z_scales_{n}", align_bytes=64)
-            quantize(z_codes[n][:], z_scales[n][:], z_values[n][:].rearrange("p n t -> p (n t)"))
+            nc.vector.quantize_mx(
+                out=z_codes[n][:].bitcast(FP8X4), scales=z_scales[n][:], in_=z[:].rearrange("p n t -> p (n t)")
+            )
+
+        w2_codes = keep.tile([P, N], U32, name="w2_codes", align_bytes=64)
+        w2_scales = keep.tile([P, N], U8, name="w2_scales", align_bytes=64)
 
         def project(n):
-            o_bank = psum.tile([P, CHUNK], F32, name=f"o_{n}", tag=f_bank_tag(n))
-            mx_pass(o_bank[:], w2_codes[:], w2_scales[:], z_codes[n][:], z_scales[n][:])
+            o_bank = psum.tile([P, CHUNK], F32, name=f"o_{n}", tag=F_BANK[n])
+            nc.tensor.matmul_mx(
+                out=o_bank[:],
+                lhsT=w2_codes[:].bitcast(FP8X4),
+                lhsT_scale=w2_scales[:],
+                rhs=z_codes[n][:].bitcast(FP8X4),
+                rhs_scale=z_scales[n][:],
+                start=True,
+                stop=True,
+            )
             result = keep.tile([P, CHUNK], F32, name=f"result_{n}")
             nc.scalar.copy(out=result[:], in_=o_bank[:])
-            nc.sync.dma_start(out=out[:, chunk(n)], in_=result[:])
+            nc.sync.dma_start(out=out[:, n * CHUNK : (n + 1) * CHUNK], in_=result[:])
 
-        for n in range(LAST):
-            product_c(n)
+        w2_grouped = keep.tile([P, N, PACK], BF16, name="w2_grouped", align_bytes=64)
 
-        round_w3()
-        round_edges(0)
-        quantize_w3(0)
-        quantize_edges(0)
-        quantize_w3(1)
-        gate(0)
+        def cast_w2(n):
+            cast_columns(w2_grouped[:], w2_raw[:], N, W2_SCALAR)
 
-        for first, count in EDGE_LOADS[1:]:
-            for n in range(first, first + count):
-                round_edges(n)
-            for n in range(first, first + count):
-                quantize_edges(n)
-                gate(n)
-        product_c(LAST)
+        def quantize_w2(n):
+            nc.vector.quantize_mx(
+                out=w2_codes[:].bitcast(FP8X4), scales=w2_scales[:], in_=w2_grouped[:].rearrange("p w t -> p (w t)")
+            )
 
-        for n in range(LAST):
-            message(n)
-        quantize_z(0)
-        quantize_z(1)
-        message(LAST)
-        round_columns(w2_rounded[:], w2_raw[:], N, N)
-        quantize(w2_codes[:], w2_scales[:], w2_rounded[:].rearrange("p w t -> p (w t)"))
-        quantize_z(2)
-        quantize_z(LAST)
-        for n in range(CHUNKS):
-            project(n)
+        steps = {"c": product_c, "a": cast_w3, "b": quantize_w3, "E": cast_edges, "Q": edges, "g": gate}
+        steps.update({"M": message, "Z": quantize_z, "p": project, "W": cast_w2, "V": quantize_w2})
+        for step in ORDER.split():
+            steps[step[0]](int(step[1:] or 0))

@@ -19,19 +19,15 @@ P = 128
 PACK = 4
 K_PASS = P * PACK
 CHUNK = 128
+CHUNKS = S // CHUNK
+LAST = CHUNKS - 1
 
-X_SCALAR = (336, 360, 800, 720)
-W1_SCALAR = (12, 46)
-W3_SCALAR = 44
-HOLDS = {3: 3}
-ORDER = "c0 c1 c2 a0 E0 b0 Q0 b1 g0 E1 Q1 g1 E2 E3 Q2 g2 Q3 g3 c3 M0 M1 M2 Z0 Z1 M3 W V Z2 Z3 p0 p1 p2 p3"
-W2_BEFORE = 4
-X_PARTS = 4
-E_LOADS = ((0, 1), (1, 1), (2, 2))
-E_SCALAR = (0, 128, 0, 0)
-W2_SCALAR = 128
-C_BANK = ("bank_0", "bank_1", "bank_2", "bank_3")
-F_BANK = ("bank_4", "bank_5", "bank_6", "bank_7")
+X_SCALAR_COLUMNS = (336, 360, 800, 720)
+W1_BOTH, W1_ALONE = 12, 46
+W3_SCALAR_ROWS = 44
+EDGE_LOADS = ((0, 1), (1, 1), (2, 2))
+SCALAR_EDGE_CHUNK = 1
+WARM_UP_PASSES = 5
 
 
 def tile_picked_schnet_sigmoid_e_kernel(tc, xT, eT, w1, w3, w2, offs, out):
@@ -40,7 +36,10 @@ def tile_picked_schnet_sigmoid_e_kernel(tc, xT, eT, w1, w3, w2, offs, out):
     def rows_of_4(dram):
         return dram.rearrange("(p j) w -> p j w", j=PACK)
 
-    def cast_columns(dst, src, width, scalar_width):
+    def chunk(n):
+        return slice(n * CHUNK, (n + 1) * CHUNK)
+
+    def round_columns(dst, src, width, scalar_width):
         dst = dst.rearrange("p (c i) t -> p c t i", i=4)
         src = src.rearrange("p t (c i) -> p c t i", i=4)
         cut = (width - scalar_width) // 4
@@ -49,228 +48,206 @@ def tile_picked_schnet_sigmoid_e_kernel(tc, xT, eT, w1, w3, w2, offs, out):
         if cut < width // 4:
             nc.scalar.copy(out=dst[:, cut:], in_=src[:, cut:])
 
-    def load(dram, shape, name):
-        raw = keep.tile(shape, F32, name=name, align_bytes=64)
-        nc.sync.dma_start(out=raw[:], in_=rows_of_4(dram))
-        return raw
+    def quantize(codes, scales, values):
+        nc.vector.quantize_mx(out=codes.bitcast(FP8X4), scales=scales, in_=values)
+
+    def mx_pass(bank, lhs_codes, lhs_scales, rhs_codes, rhs_scales, start=True, stop=True):
+        nc.tensor.matmul_mx(
+            out=bank,
+            lhsT=lhs_codes.bitcast(FP8X4),
+            lhsT_scale=lhs_scales,
+            rhs=rhs_codes.bitcast(FP8X4),
+            rhs_scale=rhs_scales,
+            start=start,
+            stop=stop,
+        )
 
     with ExitStack() as ctx:
         keep = ctx.enter_context(tc.tile_pool(name="keep", bufs=1))
         psum = ctx.enter_context(tc.psum_pool(name="psum", bufs=1))
 
-        offsets = keep.tile([P, S // 16], U16, name="offsets")
-        def load_pair(s, u):
+        def load(dram, shape, name):
+            raw = keep.tile(shape, F32, name=name, align_bytes=64)
+            nc.sync.dma_start(out=raw[:], in_=rows_of_4(dram))
+            return raw
+
+        def load_row_pair(s, u):
             raw = keep.tile([P, 2, T], F32, name=f"x_raw_{s}_{u}", align_bytes=64)
-            rows = xT[s * K_PASS : (s + 1) * K_PASS, :].rearrange("(p j) w -> p j w", j=PACK)
+            rows = rows_of_4(xT[s * K_PASS : (s + 1) * K_PASS, :])
             nc.sync.dma_start(out=raw[:], in_=rows[:, 2 * u : 2 * u + 2, :])
             return raw
 
-        x_raw = [load_pair(0, 0)]
+        offsets = keep.tile([P, S // 16], U16, name="offsets")
+        x_raw = [load_row_pair(0, 0)]
         nc.sync.dma_start(offsets[:], offs)
-        x_raw.extend([load_pair(0, 1), load_pair(1, 0), load_pair(1, 1)])
+        x_raw.extend([load_row_pair(0, 1), load_row_pair(1, 0), load_row_pair(1, 1)])
         w1_raw = keep.tile([P, 2, PACK, H], F32, name="w1_raw", align_bytes=64)
         for s in range(2):
             nc.sync.dma_start(out=w1_raw[:, s], in_=rows_of_4(w1[s * K_PASS : (s + 1) * K_PASS, :]))
         w3_raw = load(w3, [P, PACK, H], "w3_raw")
         e_raw = []
-        for first, count in E_LOADS:
-            if first == W2_BEFORE:
-                w2_raw = load(w2, [P, PACK, N], "w2_raw")
+        for first, count in EDGE_LOADS:
             raw = load(eT[:, first * CHUNK : (first + count) * CHUNK], [P, PACK, count * CHUNK], f"e_raw_{first}")
-            e_raw.extend([raw[:, :, q * CHUNK : (q + 1) * CHUNK] for q in range(count)])
-        if W2_BEFORE == 4:
-            w2_raw = load(w2, [P, PACK, N], "w2_raw")
+            e_raw.extend([raw[:, :, chunk(q)] for q in range(count)])
+        w2_raw = load(w2, [P, PACK, N], "w2_raw")
 
         warm = keep.tile([P, 1], F32, name="warm")
         nc.vector.memset(warm[:], 0.0)
         nc.scalar.activation(out=warm[:], in_=warm[:], func=SIGMOID)
 
-        g_codes = [keep.tile([P, S], U32, name=f"g_codes_{s}", align_bytes=64) for s in range(2)]
-        g_scales_0 = keep.tile([P, S], U8, name="g_scales_0", align_bytes=64)
-        planes = keep.tile([P, S], U8, name="planes", align_bytes=64)
+        x_codes = [keep.tile([P, S], U32, name=f"x_codes_{s}", align_bytes=64) for s in range(2)]
+        x_scales = [keep.tile([P, S], U8, name=f"x_scales_{s}", align_bytes=64) for s in range(2)]
 
         def pick_atoms(s):
-            halves = keep.tile([P, 2, S], U32, name=f"halves_{s}", align_bytes=64)
+            words = keep.tile([P, 2, S], U32, name=f"words_{s}", align_bytes=64)
             picked = keep.tile([P, S, 2], U32, name=f"picked_{s}", align_bytes=64)
-            parts = [slice(q * S // X_PARTS, (q + 1) * S // X_PARTS) for q in range(X_PARTS)]
+            parts = [chunk(n) for n in range(CHUNKS)]
             for u in range(2):
                 pairs = keep.tile([P, T, 2], BF16, name=f"pairs_{s}_{u}", align_bytes=64)
-                cast_columns(pairs[:], x_raw[2 * s + u][:], T, X_SCALAR[2 * s + u])
+                round_columns(pairs[:], x_raw[2 * s + u][:], T, X_SCALAR_COLUMNS[2 * s + u])
                 window = pairs[:].rearrange("p w e -> p (w e)").bitcast(U32)
                 for part in parts:
                     listed = offsets[:, part.start // 16 : part.stop // 16]
-                    nc.vector.tensor_copy(out=halves[:, u, part], in_=window.indirect(listed))
+                    nc.vector.tensor_copy(out=words[:, u, part], in_=window.indirect(listed))
             for part in parts:
                 dst = picked[:, part, :].bitcast(I32).rearrange("p (c i) u -> p c u i", i=2)
-                src = halves[:, :, part].bitcast(I32).rearrange("p u (c i) -> p c u i", i=2)
+                src = words[:, :, part].bitcast(I32).rearrange("p u (c i) -> p c u i", i=2)
                 nc.vector.tensor_copy(out=dst, in_=src)
-            scales = g_scales_0 if s == 0 else planes
             for part in parts:
-                nc.vector.quantize_mx(
-                    out=g_codes[s][:, part].bitcast(FP8X4),
-                    scales=scales[:, part],
-                    in_=picked[:, part, :].rearrange("p n u -> p (n u)").bitcast(BF16),
-                )
+                values = picked[:, part, :].rearrange("p n u -> p (n u)").bitcast(BF16)
+                quantize(x_codes[s][:, part], x_scales[s][:, part], values)
 
         pick_atoms(0)
         pick_atoms(1)
 
-        idle_bank = psum.tile([P, 2, 2 * CHUNK], F32, name="idle_bank", tag=F_BANK[3])
-        for i in range(5):
-            nc.tensor.matmul_mx(
-                out=idle_bank[:, i % 2, :],
-                lhsT=g_codes[1][:, 2 * CHUNK : 3 * CHUNK].bitcast(FP8X4),
-                lhsT_scale=planes[:, 2 * CHUNK : 3 * CHUNK],
-                rhs=g_codes[1][:, 2 * CHUNK :].bitcast(FP8X4),
-                rhs_scale=planes[:, 2 * CHUNK :],
-                start=True,
-                stop=True,
+        def c_bank_tag(n):
+            return f"bank_{n}"
+
+        def f_bank_tag(n):
+            return f"bank_{CHUNKS + n}"
+
+        idle_bank = psum.tile([P, 2, 2 * CHUNK], F32, name="idle_bank", tag=f_bank_tag(LAST))
+        for i in range(WARM_UP_PASSES):
+            mx_pass(
+                idle_bank[:, i % 2, :],
+                x_codes[1][:, chunk(2)],
+                x_scales[1][:, chunk(2)],
+                x_codes[1][:, 2 * CHUNK :],
+                x_scales[1][:, 2 * CHUNK :],
             )
 
         w1_codes = keep.tile([P, 2, H], U32, name="w1_codes", align_bytes=64)
         w1_scales = keep.tile([P, 2, H], U8, name="w1_scales", align_bytes=64)
-        w1_grouped = keep.tile([P, 2, PACK, P, PACK], BF16, name="w1_grouped", align_bytes=64)
-        dst = w1_grouped[:].rearrange("p s t m j -> p s m j t")
+        w1_dealt = keep.tile([P, 2, PACK, P, PACK], BF16, name="w1_dealt", align_bytes=64)
+        dst = w1_dealt[:].rearrange("p s t m j -> p s m j t")
         src = w1_raw[:].rearrange("p s j (m t) -> p s m j t", t=PACK)
-        both, alone = W1_SCALAR
-        nc.scalar.copy(out=dst[:, 0, both:], in_=src[:, 0, both:])
-        nc.vector.tensor_copy(out=dst[:, 1, both + alone :], in_=src[:, 1, both + alone :])
-        nc.scalar.copy(out=dst[:, :, :both], in_=src[:, :, :both])
-        nc.scalar.copy(out=dst[:, 1, both : both + alone], in_=src[:, 1, both : both + alone])
+        cut = W1_BOTH + W1_ALONE
+        nc.scalar.copy(out=dst[:, 0, W1_BOTH:], in_=src[:, 0, W1_BOTH:])
+        nc.vector.tensor_copy(out=dst[:, 1, cut:], in_=src[:, 1, cut:])
+        nc.scalar.copy(out=dst[:, :, :W1_BOTH], in_=src[:, :, :W1_BOTH])
+        nc.scalar.copy(out=dst[:, 1, W1_BOTH:cut], in_=src[:, 1, W1_BOTH:cut])
         for s in range(2):
-            nc.vector.quantize_mx(
-                out=w1_codes[:, s, :].bitcast(FP8X4),
-                scales=w1_scales[:, s, :],
-                in_=w1_grouped[:, s].rearrange("p t m j -> p (t m j)"),
-            )
+            quantize(w1_codes[:, s, :], w1_scales[:, s, :], w1_dealt[:, s].rearrange("p t m j -> p (t m j)"))
+
         w3_codes = keep.tile([P, H], U32, name="w3_codes", align_bytes=64)
         w3_scales = keep.tile([P, H], U8, name="w3_scales", align_bytes=64)
-        w3_grouped = keep.tile([P, PACK, P, PACK], BF16, name="w3_grouped", align_bytes=64)
-        slots = PACK // 2
+        w3_dealt = keep.tile([P, PACK, P, PACK], BF16, name="w3_dealt", align_bytes=64)
+        w2_codes = keep.tile([P, N], U32, name="w2_codes", align_bytes=64)
+        w2_scales = keep.tile([P, N], U8, name="w2_scales", align_bytes=64)
+        w2_rounded = keep.tile([P, N, PACK], BF16, name="w2_rounded", align_bytes=64)
+        c_banks, e_rounded, e_codes, e_scales, gates, z_values, z_codes, z_scales = [{} for name in range(8)]
 
-        def cast_w3(h):
-            dst = w3_grouped[:].rearrange("p t m j -> p m j t")
-            src = w3_raw[:].rearrange("p j (m t) -> p m j t", t=PACK)
-            cut = W3_SCALAR
-            if cut > 0:
-                nc.scalar.copy(out=dst[:, :cut], in_=src[:, :cut])
-            if cut < P:
-                nc.vector.tensor_copy(out=dst[:, cut:], in_=src[:, cut:])
+        def slot(t):
+            return slice(t * P, (t + 1) * P)
+
+        def round_w3():
+            dealt = w3_dealt[:].rearrange("p t m j -> p m j t")
+            raw = w3_raw[:].rearrange("p j (m t) -> p m j t", t=PACK)
+            nc.scalar.copy(out=dealt[:, :W3_SCALAR_ROWS], in_=raw[:, :W3_SCALAR_ROWS])
+            nc.vector.tensor_copy(out=dealt[:, W3_SCALAR_ROWS:], in_=raw[:, W3_SCALAR_ROWS:])
 
         def quantize_w3(h):
-            cols = slice(h * slots * P, (h + 1) * slots * P)
-            nc.vector.quantize_mx(
-                out=w3_codes[:, cols].bitcast(FP8X4),
-                scales=w3_scales[:, cols],
-                in_=w3_grouped[:, h * slots : (h + 1) * slots].rearrange("p t m j -> p (t m j)"),
-            )
-
-        c_banks = {}
+            cols = slice(2 * h * P, 2 * (h + 1) * P)
+            values = w3_dealt[:, 2 * h : 2 * (h + 1)].rearrange("p t m j -> p (t m j)")
+            quantize(w3_codes[:, cols], w3_scales[:, cols], values)
 
         def product_c(n):
-            cols = slice(n * CHUNK, (n + 1) * CHUNK)
-            c_banks[n] = psum.tile([P, PACK, CHUNK], F32, name=f"c_{n}", tag=C_BANK[n])
+            c_banks[n] = psum.tile([P, PACK, CHUNK], F32, name=f"c_{n}", tag=c_bank_tag(n))
             for t in range(PACK):
-                rows = slice(t * P, (t + 1) * P)
                 for s in range(2):
-                    nc.tensor.matmul_mx(
-                        out=c_banks[n][:, t, :],
-                        lhsT=w1_codes[:, s, rows].bitcast(FP8X4),
-                        lhsT_scale=w1_scales[:, s, rows],
-                        rhs=g_codes[s][:, cols].bitcast(FP8X4),
-                        rhs_scale=(g_scales_0 if s == 0 else planes)[:, cols],
+                    mx_pass(
+                        c_banks[n][:, t, :],
+                        w1_codes[:, s, slot(t)],
+                        w1_scales[:, s, slot(t)],
+                        x_codes[s][:, chunk(n)],
+                        x_scales[s][:, chunk(n)],
                         start=(s == 0),
                         stop=(s == 1),
                     )
 
-        e_codes = {}
-        e_scales = {}
+        def round_edges(n):
+            e_rounded[n] = keep.tile([P, CHUNK, PACK], BF16, name=f"e_rounded_{n}", align_bytes=64)
+            round_columns(e_rounded[n][:], e_raw[n], CHUNK, CHUNK if n == SCALAR_EDGE_CHUNK else 0)
 
-        e_grouped = {}
-
-        def cast_edges(n):
-            e_grouped[n] = keep.tile([P, CHUNK, PACK], BF16, name=f"e_grouped_{n}", align_bytes=64)
-            cast_columns(e_grouped[n][:], e_raw[n], CHUNK, E_SCALAR[n])
-
-        def edges(n):
-            grouped = e_grouped[n]
+        def quantize_edges(n):
             e_codes[n] = keep.tile([P, CHUNK], U32, name=f"e_codes_{n}", align_bytes=64)
-            if n in HOLDS:
-                e_scales[n] = planes[4:P, HOLDS[n] * CHUNK : (HOLDS[n] + 1) * CHUNK]
+            if n == LAST:
+                e_scales[n] = x_scales[1][4:P, chunk(n)]
             else:
                 own = keep.tile([P, CHUNK], U8, name=f"e_scales_{n}", align_bytes=64)
                 e_scales[n] = own[:]
-            nc.vector.quantize_mx(
-                out=e_codes[n][:].bitcast(FP8X4), scales=e_scales[n], in_=grouped[:].rearrange("p w t -> p (w t)")
-            )
-
-        gates = {}
+            quantize(e_codes[n][:], e_scales[n], e_rounded[n][:].rearrange("p w t -> p (w t)"))
 
         def gate(n):
-            f_bank = psum.tile([P, PACK, CHUNK], F32, name=f"f_{n}", tag=F_BANK[n])
+            f_bank = psum.tile([P, PACK, CHUNK], F32, name=f"f_{n}", tag=f_bank_tag(n))
             for t in range(PACK):
-                rows = slice(t * P, (t + 1) * P)
-                nc.tensor.matmul_mx(
-                    out=f_bank[:, t, :],
-                    lhsT=w3_codes[:, rows].bitcast(FP8X4),
-                    lhsT_scale=w3_scales[:, rows],
-                    rhs=e_codes[n][:].bitcast(FP8X4),
-                    rhs_scale=e_scales[n],
-                    start=True,
-                    stop=True,
-                )
+                mx_pass(f_bank[:, t, :], w3_codes[:, slot(t)], w3_scales[:, slot(t)], e_codes[n][:], e_scales[n])
             gates[n] = keep.tile([P, CHUNK, PACK], F32, name=f"gate_{n}", align_bytes=64)
             nc.scalar.activation(out=gates[n][:], in_=f_bank[:].rearrange("p t n -> p n t"), func=SIGMOID)
 
-        z_codes = {}
-        z_scales = {}
-
-        z_tiles = {}
-
         def message(n):
-            z = keep.tile([P, CHUNK, PACK], BF16, name=f"z_{n}", align_bytes=64)
-            z_tiles[n] = z
-            nc.vector.tensor_tensor(
-                out=z[:], in0=c_banks[n][:].rearrange("p t n -> p n t"), in1=gates[n][:], op=MULT
-            )
+            z_values[n] = keep.tile([P, CHUNK, PACK], BF16, name=f"z_{n}", align_bytes=64)
+            c = c_banks[n][:].rearrange("p t n -> p n t")
+            nc.vector.tensor_tensor(out=z_values[n][:], in0=c, in1=gates[n][:], op=MULT)
 
         def quantize_z(n):
-            z = z_tiles[n]
             z_codes[n] = keep.tile([P, CHUNK], U32, name=f"z_codes_{n}", align_bytes=64)
             z_scales[n] = keep.tile([P, CHUNK], U8, name=f"z_scales_{n}", align_bytes=64)
-            nc.vector.quantize_mx(
-                out=z_codes[n][:].bitcast(FP8X4), scales=z_scales[n][:], in_=z[:].rearrange("p n t -> p (n t)")
-            )
-
-        w2_codes = keep.tile([P, N], U32, name="w2_codes", align_bytes=64)
-        w2_scales = keep.tile([P, N], U8, name="w2_scales", align_bytes=64)
+            quantize(z_codes[n][:], z_scales[n][:], z_values[n][:].rearrange("p n t -> p (n t)"))
 
         def project(n):
-            o_bank = psum.tile([P, CHUNK], F32, name=f"o_{n}", tag=F_BANK[n])
-            nc.tensor.matmul_mx(
-                out=o_bank[:],
-                lhsT=w2_codes[:].bitcast(FP8X4),
-                lhsT_scale=w2_scales[:],
-                rhs=z_codes[n][:].bitcast(FP8X4),
-                rhs_scale=z_scales[n][:],
-                start=True,
-                stop=True,
-            )
+            o_bank = psum.tile([P, CHUNK], F32, name=f"o_{n}", tag=f_bank_tag(n))
+            mx_pass(o_bank[:], w2_codes[:], w2_scales[:], z_codes[n][:], z_scales[n][:])
             result = keep.tile([P, CHUNK], F32, name=f"result_{n}")
             nc.scalar.copy(out=result[:], in_=o_bank[:])
-            nc.sync.dma_start(out=out[:, n * CHUNK : (n + 1) * CHUNK], in_=result[:])
+            nc.sync.dma_start(out=out[:, chunk(n)], in_=result[:])
 
-        w2_grouped = keep.tile([P, N, PACK], BF16, name="w2_grouped", align_bytes=64)
+        for n in range(LAST):
+            product_c(n)
 
-        def cast_w2(n):
-            cast_columns(w2_grouped[:], w2_raw[:], N, W2_SCALAR)
+        round_w3()
+        round_edges(0)
+        quantize_w3(0)
+        quantize_edges(0)
+        quantize_w3(1)
+        gate(0)
 
-        def quantize_w2(n):
-            nc.vector.quantize_mx(
-                out=w2_codes[:].bitcast(FP8X4), scales=w2_scales[:], in_=w2_grouped[:].rearrange("p w t -> p (w t)")
-            )
+        for first, count in EDGE_LOADS[1:]:
+            for n in range(first, first + count):
+                round_edges(n)
+            for n in range(first, first + count):
+                quantize_edges(n)
+                gate(n)
+        product_c(LAST)
 
-        steps = {"c": product_c, "a": cast_w3, "b": quantize_w3, "E": cast_edges, "Q": edges, "g": gate}
-        steps.update({"M": message, "Z": quantize_z, "p": project, "W": cast_w2, "V": quantize_w2})
-        for step in ORDER.split():
-            steps[step[0]](int(step[1:] or 0))
+        for n in range(LAST):
+            message(n)
+        quantize_z(0)
+        quantize_z(1)
+        message(LAST)
+        round_columns(w2_rounded[:], w2_raw[:], N, N)
+        quantize(w2_codes[:], w2_scales[:], w2_rounded[:].rearrange("p w t -> p (w t)"))
+        quantize_z(2)
+        quantize_z(LAST)
+        for n in range(CHUNKS):
+            project(n)

@@ -22,12 +22,14 @@ CHUNK = 128
 CHUNKS = S // CHUNK
 LAST = CHUNKS - 1
 
-X_SCALAR_COLUMNS = (336, 360, 800, 720)
-W1_BOTH, W1_ALONE = 12, 46
+X_SCALAR_COLUMNS = (336, 360, 728, 592)
+W1_SCALAR_ROWS = ((128, 88), (64, 52))
+HELD_BY = {1: 2, 3: 3}
 W3_SCALAR_ROWS = 44
 EDGE_LOADS = ((0, 1), (1, 1), (2, 2))
 SCALAR_EDGE_CHUNK = 1
 WARM_UP_PASSES = 5
+EDGE = 144
 
 
 def tile_picked_schnet_sigmoid_e_kernel(tc, xT, eT, w1, w3, w2, offs, out):
@@ -80,10 +82,14 @@ def tile_picked_schnet_sigmoid_e_kernel(tc, xT, eT, w1, w3, w2, offs, out):
         offsets = keep.tile([P, S // 16], U16, name="offsets")
         x_raw = [load_row_pair(0, 0)]
         nc.sync.dma_start(offsets[:], offs)
-        x_raw.extend([load_row_pair(0, 1), load_row_pair(1, 0), load_row_pair(1, 1)])
-        w1_raw = keep.tile([P, 2, PACK, H], F32, name="w1_raw", align_bytes=64)
-        for s in range(2):
-            nc.sync.dma_start(out=w1_raw[:, s], in_=rows_of_4(w1[s * K_PASS : (s + 1) * K_PASS, :]))
+        x_raw.append(load_row_pair(0, 1))
+        margin = S - EDGE
+        shared = keep.tile([P, 2 * T + 2 * margin], F32, name="x_raw_1_0", align_bytes=64)
+        rows = rows_of_4(xT[K_PASS:, :])[:, 0:2, :].rearrange("p j w -> p (j w)")
+        nc.sync.dma_start(out=shared[:, margin : margin + 2 * T], in_=rows)
+        x_raw.append(shared[:, margin : margin + 2 * T].rearrange("p (j w) -> p j w", j=2))
+        x_raw.append(load_row_pair(1, 1))
+        w1_raw = [load(w1[s * K_PASS : (s + 1) * K_PASS, :], [P, PACK, H], f"w1_raw_{s}") for s in range(2)]
         w3_raw = load(w3, [P, PACK, H], "w3_raw")
         e_raw = []
         for first, count in EDGE_LOADS:
@@ -100,25 +106,40 @@ def tile_picked_schnet_sigmoid_e_kernel(tc, xT, eT, w1, w3, w2, offs, out):
 
         def pick_atoms(s):
             words = keep.tile([P, 2, S], U32, name=f"words_{s}", align_bytes=64)
-            picked = keep.tile([P, S, 2], U32, name=f"picked_{s}", align_bytes=64)
-            parts = [chunk(n) for n in range(CHUNKS)]
+            if s == 0:
+                halves = [shared[:, :S], shared[:, 2 * T + 2 * margin - S :]]
+            else:
+                own = keep.tile([P, 2 * S], F32, name="picked_1", align_bytes=64)
+                halves = [own[:, :S], own[:, S:]]
+            parts = [slice(0, S // 2), slice(S // 2, S)]
             for u in range(2):
                 pairs = keep.tile([P, T, 2], BF16, name=f"pairs_{s}_{u}", align_bytes=64)
-                round_columns(pairs[:], x_raw[2 * s + u][:], T, X_SCALAR_COLUMNS[2 * s + u])
+                if (s, u) == (1, 0):
+                    for cols in (slice(0, EDGE), slice(T - EDGE, T)):
+                        round_columns(pairs[:, cols], x_raw[2][:, :, cols], EDGE, 0)
+                    round_columns(pairs[:, EDGE : T - EDGE], x_raw[2][:, :, EDGE : T - EDGE], T - 2 * EDGE, T - 2 * EDGE)
+                    weave_and_quantize[0]()
+                else:
+                    round_columns(pairs[:], x_raw[2 * s + u][:], T, X_SCALAR_COLUMNS[2 * s + u])
                 window = pairs[:].rearrange("p w e -> p (w e)").bitcast(U32)
                 for part in parts:
                     listed = offsets[:, part.start // 16 : part.stop // 16]
                     nc.vector.tensor_copy(out=words[:, u, part], in_=window.indirect(listed))
-            for part in parts:
-                dst = picked[:, part, :].bitcast(I32).rearrange("p (c i) u -> p c u i", i=2)
-                src = words[:, :, part].bitcast(I32).rearrange("p u (c i) -> p c u i", i=2)
-                nc.vector.tensor_copy(out=dst, in_=src)
-            for part in parts:
-                values = picked[:, part, :].rearrange("p n u -> p (n u)").bitcast(BF16)
-                quantize(x_codes[s][:, part], x_scales[s][:, part], values)
 
+            def finish():
+                for part, half in zip(parts, halves):
+                    dst = half.bitcast(I32).rearrange("p (c i u) -> p c u i", i=2, u=2)
+                    src = words[:, :, part].bitcast(I32).rearrange("p u (c i) -> p c u i", i=2)
+                    nc.vector.tensor_copy(out=dst, in_=src)
+                for part, half in zip(parts, halves):
+                    quantize(x_codes[s][:, part], x_scales[s][:, part], half.bitcast(BF16))
+
+            weave_and_quantize.append(finish)
+
+        weave_and_quantize = []
         pick_atoms(0)
         pick_atoms(1)
+        weave_and_quantize[1]()
 
         def c_bank_tag(n):
             return f"bank_{n}"
@@ -136,18 +157,40 @@ def tile_picked_schnet_sigmoid_e_kernel(tc, xT, eT, w1, w3, w2, offs, out):
                 x_scales[1][:, 2 * CHUNK :],
             )
 
+        def slot(t):
+            return slice(t * P, (t + 1) * P)
+
         w1_codes = keep.tile([P, 2, H], U32, name="w1_codes", align_bytes=64)
         w1_scales = keep.tile([P, 2, H], U8, name="w1_scales", align_bytes=64)
-        w1_dealt = keep.tile([P, 2, PACK, P, PACK], BF16, name="w1_dealt", align_bytes=64)
-        dst = w1_dealt[:].rearrange("p s t m j -> p s m j t")
-        src = w1_raw[:].rearrange("p s j (m t) -> p s m j t", t=PACK)
-        cut = W1_BOTH + W1_ALONE
-        nc.scalar.copy(out=dst[:, 0, W1_BOTH:], in_=src[:, 0, W1_BOTH:])
-        nc.vector.tensor_copy(out=dst[:, 1, cut:], in_=src[:, 1, cut:])
-        nc.scalar.copy(out=dst[:, :, :W1_BOTH], in_=src[:, :, :W1_BOTH])
-        nc.scalar.copy(out=dst[:, 1, W1_BOTH:cut], in_=src[:, 1, W1_BOTH:cut])
+        c_banks = [psum.tile([P, PACK, CHUNK], F32, name=f"c_{n}", tag=c_bank_tag(n)) for n in range(CHUNKS)]
+
+        def pass_of_c(s, n):
+            for t in range(PACK):
+                mx_pass(
+                    c_banks[n][:, t, :],
+                    w1_codes[:, s, slot(t)],
+                    w1_scales[:, s, slot(t)],
+                    x_codes[s][:, chunk(n)],
+                    x_scales[s][:, chunk(n)],
+                    start=(s == 0 and t == 0),
+                    stop=(s == 1 and t == PACK - 1),
+                )
+
         for s in range(2):
-            quantize(w1_codes[:, s, :], w1_scales[:, s, :], w1_dealt[:, s].rearrange("p t m j -> p (t m j)"))
+            dealt = keep.tile([P, PACK, P, PACK], BF16, name=f"w1_dealt_{s}", align_bytes=64)
+            for h in range(2):
+                dst = dealt[:, 2 * h : 2 * h + 2].rearrange("p t m j -> p m j t")
+                src = w1_raw[s][:].rearrange("p j (m t) -> p m j t", t=PACK)[:, :, :, 2 * h : 2 * h + 2]
+                rows = W1_SCALAR_ROWS[s][h]
+                nc.scalar.copy(out=dst[:, :rows], in_=src[:, :rows])
+                if rows < P:
+                    nc.vector.tensor_copy(out=dst[:, rows:], in_=src[:, rows:])
+            for h in range(2):
+                cols = slice(2 * h * P, 2 * (h + 1) * P)
+                values = dealt[:, 2 * h : 2 * h + 2].rearrange("p t m j -> p (t m j)")
+                quantize(w1_codes[:, s, cols], w1_scales[:, s, cols], values)
+            for n in range(CHUNKS if s == 0 else 2):
+                pass_of_c(s, n)
 
         w3_codes = keep.tile([P, H], U32, name="w3_codes", align_bytes=64)
         w3_scales = keep.tile([P, H], U8, name="w3_scales", align_bytes=64)
@@ -155,10 +198,7 @@ def tile_picked_schnet_sigmoid_e_kernel(tc, xT, eT, w1, w3, w2, offs, out):
         w2_codes = keep.tile([P, N], U32, name="w2_codes", align_bytes=64)
         w2_scales = keep.tile([P, N], U8, name="w2_scales", align_bytes=64)
         w2_rounded = keep.tile([P, N, PACK], BF16, name="w2_rounded", align_bytes=64)
-        c_banks, e_rounded, e_codes, e_scales, gates, z_values, z_codes, z_scales = [{} for name in range(8)]
-
-        def slot(t):
-            return slice(t * P, (t + 1) * P)
+        e_rounded, e_codes, e_scales, gates, z_values, z_codes, z_scales = [{} for name in range(7)]
 
         def round_w3():
             dealt = w3_dealt[:].rearrange("p t m j -> p m j t")
@@ -171,28 +211,14 @@ def tile_picked_schnet_sigmoid_e_kernel(tc, xT, eT, w1, w3, w2, offs, out):
             values = w3_dealt[:, 2 * h : 2 * (h + 1)].rearrange("p t m j -> p (t m j)")
             quantize(w3_codes[:, cols], w3_scales[:, cols], values)
 
-        def product_c(n):
-            c_banks[n] = psum.tile([P, PACK, CHUNK], F32, name=f"c_{n}", tag=c_bank_tag(n))
-            for t in range(PACK):
-                for s in range(2):
-                    mx_pass(
-                        c_banks[n][:, t, :],
-                        w1_codes[:, s, slot(t)],
-                        w1_scales[:, s, slot(t)],
-                        x_codes[s][:, chunk(n)],
-                        x_scales[s][:, chunk(n)],
-                        start=(s == 0),
-                        stop=(s == 1),
-                    )
-
         def round_edges(n):
             e_rounded[n] = keep.tile([P, CHUNK, PACK], BF16, name=f"e_rounded_{n}", align_bytes=64)
             round_columns(e_rounded[n][:], e_raw[n], CHUNK, CHUNK if n == SCALAR_EDGE_CHUNK else 0)
 
         def quantize_edges(n):
             e_codes[n] = keep.tile([P, CHUNK], U32, name=f"e_codes_{n}", align_bytes=64)
-            if n == LAST:
-                e_scales[n] = x_scales[1][4:P, chunk(n)]
+            if n in HELD_BY:
+                e_scales[n] = x_scales[1][4:P, chunk(HELD_BY[n])]
             else:
                 own = keep.tile([P, CHUNK], U8, name=f"e_scales_{n}", align_bytes=64)
                 e_scales[n] = own[:]
@@ -222,9 +248,6 @@ def tile_picked_schnet_sigmoid_e_kernel(tc, xT, eT, w1, w3, w2, offs, out):
             nc.scalar.copy(out=result[:], in_=o_bank[:])
             nc.sync.dma_start(out=out[:, chunk(n)], in_=result[:])
 
-        for n in range(LAST):
-            product_c(n)
-
         round_w3()
         round_edges(0)
         quantize_w3(0)
@@ -238,7 +261,8 @@ def tile_picked_schnet_sigmoid_e_kernel(tc, xT, eT, w1, w3, w2, offs, out):
             for n in range(first, first + count):
                 quantize_edges(n)
                 gate(n)
-        product_c(LAST)
+                if n in HELD_BY:
+                    pass_of_c(1, HELD_BY[n])
 
         for n in range(LAST):
             message(n)

@@ -28,7 +28,6 @@ HELD_BY = {1: 2, 3: 3}
 W3_SCALAR_ROWS = 44
 EDGE_LOADS = ((0, 1), (1, 1), (2, 2))
 SCALAR_EDGE_CHUNK = 1
-WARM_UP_PASSES = 5
 EDGE = 144
 
 
@@ -146,16 +145,6 @@ def tile_picked_schnet_sigmoid_e_kernel(tc, xT, eT, w1, w3, w2, offs, out):
 
         def f_bank_tag(n):
             return f"bank_{CHUNKS + n}"
-
-        idle_bank = psum.tile([P, 2, 2 * CHUNK], F32, name="idle_bank", tag=f_bank_tag(LAST))
-        for i in range(WARM_UP_PASSES):
-            mx_pass(
-                idle_bank[:, i % 2, :],
-                x_codes[1][:, chunk(2)],
-                x_scales[1][:, chunk(2)],
-                x_codes[1][:, 2 * CHUNK :],
-                x_scales[1][:, 2 * CHUNK :],
-            )
 
         def slot(t):
             return slice(t * P, (t + 1) * P)

@@ -25,9 +25,9 @@ LAST = CHUNKS - 1
 X_SCALAR_COLUMNS = (336, 360, 728, 592)
 W1_SCALAR_ROWS = ((128, 88), (64, 52))
 HELD_BY = {1: 2, 3: 3}
-W3_SCALAR_ROWS = 44
-EDGE_LOADS = ((0, 1), (1, 1), (2, 2))
-SCALAR_EDGE_CHUNK = 1
+W3_SCALAR_ROWS = 64
+EDGE_LOADS = ((0, 1), (1, 1), (2, 1), (3, 1))
+E_SCALAR_COLUMNS = (88, 128, 96, 0)
 EDGE = 144
 
 
@@ -183,26 +183,23 @@ def tile_picked_schnet_sigmoid_e_kernel(tc, xT, eT, w1, w3, w2, offs, out):
 
         w3_codes = keep.tile([P, H], U32, name="w3_codes", align_bytes=64)
         w3_scales = keep.tile([P, H], U8, name="w3_scales", align_bytes=64)
-        w3_dealt = keep.tile([P, PACK, P, PACK], BF16, name="w3_dealt", align_bytes=64)
+        w3_pairs = [keep.tile([P, 2, P, PACK], BF16, name=f"w3_pair_{h}", align_bytes=64)[:] for h in range(2)]
         w2_codes = keep.tile([P, N], U32, name="w2_codes", align_bytes=64)
         w2_scales = keep.tile([P, N], U8, name="w2_scales", align_bytes=64)
         w2_rounded = keep.tile([P, N, PACK], BF16, name="w2_rounded", align_bytes=64)
         e_rounded, e_codes, e_scales, gates, z_values, z_codes, z_scales = [{} for name in range(7)]
 
-        def round_w3():
-            dealt = w3_dealt[:].rearrange("p t m j -> p m j t")
-            raw = w3_raw[:].rearrange("p j (m t) -> p m j t", t=PACK)
-            nc.scalar.copy(out=dealt[:, :W3_SCALAR_ROWS], in_=raw[:, :W3_SCALAR_ROWS])
-            nc.vector.tensor_copy(out=dealt[:, W3_SCALAR_ROWS:], in_=raw[:, W3_SCALAR_ROWS:])
+        def round_w3(engine_copy, h, rows):
+            raw = w3_raw[:].rearrange("p j (m t) -> p m j t", t=PACK)[:, rows, :, 2 * h : 2 * h + 2]
+            engine_copy(out=w3_pairs[h].rearrange("p t m j -> p m j t")[:, rows], in_=raw)
 
         def quantize_w3(h):
             cols = slice(2 * h * P, 2 * (h + 1) * P)
-            values = w3_dealt[:, 2 * h : 2 * (h + 1)].rearrange("p t m j -> p (t m j)")
-            quantize(w3_codes[:, cols], w3_scales[:, cols], values)
+            quantize(w3_codes[:, cols], w3_scales[:, cols], w3_pairs[h].rearrange("p t m j -> p (t m j)"))
 
         def round_edges(n):
             e_rounded[n] = keep.tile([P, CHUNK, PACK], BF16, name=f"e_rounded_{n}", align_bytes=64)
-            round_columns(e_rounded[n][:], e_raw[n], CHUNK, CHUNK if n == SCALAR_EDGE_CHUNK else 0)
+            round_columns(e_rounded[n][:], e_raw[n], CHUNK, E_SCALAR_COLUMNS[n])
 
         def quantize_edges(n):
             e_codes[n] = keep.tile([P, CHUNK], U32, name=f"e_codes_{n}", align_bytes=64)
@@ -213,53 +210,74 @@ def tile_picked_schnet_sigmoid_e_kernel(tc, xT, eT, w1, w3, w2, offs, out):
                 e_scales[n] = own[:]
             quantize(e_codes[n][:], e_scales[n], e_rounded[n][:].rearrange("p w t -> p (w t)"))
 
+        def f_passes(bank, n, slots):
+            for i, t in enumerate(slots):
+                mx_pass(bank[:, i, :], w3_codes[:, slot(t)], w3_scales[:, slot(t)], e_codes[n][:], e_scales[n])
+
         def gate(n):
             f_bank = psum.tile([P, PACK, CHUNK], F32, name=f"f_{n}", tag=f_bank_tag(n))
-            for t in range(PACK):
-                mx_pass(f_bank[:, t, :], w3_codes[:, slot(t)], w3_scales[:, slot(t)], e_codes[n][:], e_scales[n])
-            gates[n] = keep.tile([P, CHUNK, PACK], F32, name=f"gate_{n}", align_bytes=64)
-            nc.scalar.activation(out=gates[n][:], in_=f_bank[:].rearrange("p t n -> p n t"), func=SIGMOID)
+            f_passes(f_bank, n, range(PACK))
+            tile = keep.tile([P, CHUNK, PACK], F32, name=f"gate_{n}", align_bytes=64)
+            nc.scalar.activation(out=tile[:], in_=f_bank[:].rearrange("p t n -> p n t"), func=SIGMOID)
+            gates[n] = tile[:].rearrange("p n (h e) -> p n h e", e=2)
+
+        first_gate = keep.tile([P, 2, CHUNK, 2], F32, name="gate_0", align_bytes=64)
+        gates[0] = first_gate[:].rearrange("p h n e -> p n h e")
+
+        def half_gate(h):
+            f_bank = psum.tile([P, 2, CHUNK], F32, name=f"f_0_{h}", tag=f_bank_tag(h * LAST))
+            f_passes(f_bank, 0, (2 * h, 2 * h + 1))
+            nc.scalar.activation(out=first_gate[:, h], in_=f_bank[:].rearrange("p t n -> p n t"), func=SIGMOID)
 
         def message(n):
             z_values[n] = keep.tile([P, CHUNK, PACK], BF16, name=f"z_{n}", align_bytes=64)
-            c = c_banks[n][:].rearrange("p t n -> p n t")
-            nc.vector.tensor_tensor(out=z_values[n][:], in0=c, in1=gates[n][:], op=MULT)
+            c = c_banks[n][:].rearrange("p (h e) n -> p n h e", e=2)
+            z = z_values[n][:].rearrange("p n (h e) -> p n h e", e=2)
+            nc.vector.tensor_tensor(out=z, in0=c, in1=gates[n], op=MULT)
 
         def quantize_z(n):
             z_codes[n] = keep.tile([P, CHUNK], U32, name=f"z_codes_{n}", align_bytes=64)
             z_scales[n] = keep.tile([P, CHUNK], U8, name=f"z_scales_{n}", align_bytes=64)
             quantize(z_codes[n][:], z_scales[n][:], z_values[n][:].rearrange("p n t -> p (n t)"))
 
-        def project(n):
-            o_bank = psum.tile([P, CHUNK], F32, name=f"o_{n}", tag=f_bank_tag(n))
-            mx_pass(o_bank[:], w2_codes[:], w2_scales[:], z_codes[n][:], z_scales[n][:])
-            result = keep.tile([P, CHUNK], F32, name=f"result_{n}")
-            nc.scalar.copy(out=result[:], in_=o_bank[:])
-            nc.sync.dma_start(out=out[:, chunk(n)], in_=result[:])
+        result = keep.tile([P, S], F32, name="result")
 
-        round_w3()
+        def project(n):
+            o_bank = psum.tile([P, CHUNK], F32, name=f"o_{n}", tag=f_bank_tag(LAST - n))
+            mx_pass(o_bank[:], w2_codes[:], w2_scales[:], z_codes[n][:], z_scales[n][:])
+            nc.scalar.copy(out=result[:, chunk(n)], in_=o_bank[:])
+            if n > 0:
+                cols = slice(0, 2 * CHUNK) if n == 1 else chunk(n)
+                nc.sync.dma_start(out=out[:, cols], in_=result[:, cols])
+
+        round_w3(nc.scalar.copy, 0, slice(0, W3_SCALAR_ROWS))
+        round_w3(nc.vector.tensor_copy, 0, slice(W3_SCALAR_ROWS, P))
+        round_w3(nc.vector.tensor_copy, 1, slice(0, P))
         round_edges(0)
+        round_edges(1)
         quantize_w3(0)
         quantize_edges(0)
+        half_gate(0)
         quantize_w3(1)
-        gate(0)
-
-        for first, count in EDGE_LOADS[1:]:
-            for n in range(first, first + count):
-                round_edges(n)
-            for n in range(first, first + count):
-                quantize_edges(n)
-                gate(n)
-                if n in HELD_BY:
-                    pass_of_c(1, HELD_BY[n])
-
-        for n in range(LAST):
-            message(n)
-        quantize_z(0)
-        quantize_z(1)
-        message(LAST)
+        half_gate(1)
+        round_edges(2)
+        quantize_edges(1)
+        gate(1)
+        pass_of_c(1, HELD_BY[1])
+        round_edges(LAST)
+        quantize_edges(2)
+        gate(2)
+        quantize_edges(LAST)
         round_columns(w2_rounded[:], w2_raw[:], N, N)
+        gate(LAST)
+        pass_of_c(1, HELD_BY[LAST])
+        message(0)
+        message(1)
+        quantize_z(0)
+        message(2)
+        quantize_z(1)
         quantize(w2_codes[:], w2_scales[:], w2_rounded[:].rearrange("p w t -> p (w t)"))
+        message(LAST)
         quantize_z(2)
         quantize_z(LAST)
         for n in range(CHUNKS):

@@ -27,7 +27,7 @@ W1_SCALAR_ROWS = ((128, 88), (64, 52))
 HELD_BY = {1: 2, 3: 3}
 W3_SCALAR_ROWS = 64
 EDGE_LOADS = ((0, 1), (1, 1), (2, 1), (3, 1))
-E_SCALAR_COLUMNS = (88, 128, 96, 0)
+E_SCALAR_COLUMNS = (88, 128, 0, 64)
 EDGE = 144
 
 
@@ -68,7 +68,7 @@ def tile_picked_schnet_sigmoid_e_kernel(tc, xT, eT, w1, w3, w2, offs, out):
         psum = ctx.enter_context(tc.psum_pool(name="psum", bufs=1))
 
         def load(dram, shape, name):
-            raw = keep.tile(shape, F32, name=name, align_bytes=64)
+            raw = keep.tile(shape, F32, name=name, tag=name, align_bytes=64)
             nc.sync.dma_start(out=raw[:], in_=rows_of_4(dram))
             return raw
 
@@ -198,7 +198,7 @@ def tile_picked_schnet_sigmoid_e_kernel(tc, xT, eT, w1, w3, w2, offs, out):
             quantize(w3_codes[:, cols], w3_scales[:, cols], w3_pairs[h].rearrange("p t m j -> p (t m j)"))
 
         def round_edges(n):
-            e_rounded[n] = keep.tile([P, CHUNK, PACK], BF16, name=f"e_rounded_{n}", align_bytes=64)
+            e_rounded[n] = keep.tile([P, CHUNK, PACK], BF16, name=f"e_rounded_{n}", tag="e_raw_1" if n == 2 else f"e_rounded_{n}", align_bytes=64)
             round_columns(e_rounded[n][:], e_raw[n], CHUNK, E_SCALAR_COLUMNS[n])
 
         def quantize_edges(n):
@@ -260,18 +260,18 @@ def tile_picked_schnet_sigmoid_e_kernel(tc, xT, eT, w1, w3, w2, offs, out):
         half_gate(0)
         quantize_w3(1)
         half_gate(1)
-        round_edges(2)
         quantize_edges(1)
+        round_edges(2)
+        round_edges(LAST)
         gate(1)
         pass_of_c(1, HELD_BY[1])
-        round_edges(LAST)
         quantize_edges(2)
         gate(2)
+        message(0)
         quantize_edges(LAST)
         round_columns(w2_rounded[:], w2_raw[:], N, N)
         gate(LAST)
         pass_of_c(1, HELD_BY[LAST])
-        message(0)
         message(1)
         quantize_z(0)
         message(2)

@@ -41,12 +41,13 @@ def tile_picked_schnet_sigmoid_e_kernel(tc, xT, eT, w1, w3, w2, offs, out):
         return slice(n * CHUNK, (n + 1) * CHUNK)
 
     def round_columns(dst, src, width, scalar_width):
-        dst = dst.rearrange("p (c i) t -> p c t i", i=4)
-        src = src.rearrange("p t (c i) -> p c t i", i=4)
-        cut = (width - scalar_width) // 4
+        run = 8 // dst.shape[2]
+        dst = dst.rearrange("p (c i) t -> p c t i", i=run)
+        src = src.rearrange("p t (c i) -> p c t i", i=run)
+        cut = (width - scalar_width) // run
         if cut > 0:
             nc.vector.tensor_copy(out=dst[:, :cut], in_=src[:, :cut])
-        if cut < width // 4:
+        if cut < width // run:
             nc.scalar.copy(out=dst[:, cut:], in_=src[:, cut:])
 
     def quantize(codes, scales, values):

from contextlib import ExitStack

import concourse.mybir as mybir

F32 = mybir.dt.float32
BF16 = mybir.dt.bfloat16
U32 = mybir.dt.uint32
I32 = mybir.dt.int32
U16 = mybir.dt.uint16
U8 = mybir.dt.uint8
FP8X4 = mybir.dt.float8_e4m3fn_x4
SIGMOID = mybir.ActivationFunctionType.Sigmoid
MULT = mybir.AluOpType.mult

K, T, S, J, H, N = 1024, 1024, 512, 512, 512, 128
FLOPS = 2 * S * (K * H + J * H + H * N)

P = 128
PACK = 4
K_PASS = P * PACK
CHUNK = 128
CHUNKS = S // CHUNK
LAST = CHUNKS - 1

X_SCALAR_COLUMNS = (336, 360, 728, 592)
W1_SCALAR_ROWS = ((128, 88), (64, 52))
HELD_BY = {1: 2, 3: 3}
W3_SCALAR_ROWS = 64
EDGE_LOADS = ((0, 1), (1, 1), (2, 1), (3, 1))
E_SCALAR_COLUMNS = (88, 128, 0, 64)
EDGE = 144


def tile_picked_schnet_sigmoid_e_kernel(tc, xT, eT, w1, w3, w2, offs, out):
    nc = tc.nc

    def rows_of_4(dram):
        return dram.rearrange("(p j) w -> p j w", j=PACK)

    def chunk(n):
        return slice(n * CHUNK, (n + 1) * CHUNK)

    def round_columns(dst, src, width, scalar_width):
        run = 8 // dst.shape[2]
        dst = dst.rearrange("p (c i) t -> p c t i", i=run)
        src = src.rearrange("p t (c i) -> p c t i", i=run)
        cut = (width - scalar_width) // run
        if cut > 0:
            nc.vector.tensor_copy(out=dst[:, :cut], in_=src[:, :cut])
        if cut < width // run:
            nc.scalar.copy(out=dst[:, cut:], in_=src[:, cut:])

    def quantize(codes, scales, values):
        nc.vector.quantize_mx(out=codes.bitcast(FP8X4), scales=scales, in_=values)

    def mx_pass(bank, lhs_codes, lhs_scales, rhs_codes, rhs_scales, start=True, stop=True):
        nc.tensor.matmul_mx(
            out=bank,
            lhsT=lhs_codes.bitcast(FP8X4),
            lhsT_scale=lhs_scales,
            rhs=rhs_codes.bitcast(FP8X4),
            rhs_scale=rhs_scales,
            start=start,
            stop=stop,
        )

    with ExitStack() as ctx:
        keep = ctx.enter_context(tc.tile_pool(name="keep", bufs=1))
        psum = ctx.enter_context(tc.psum_pool(name="psum", bufs=1))

        def load(dram, shape, name):
            raw = keep.tile(shape, F32, name=name, tag=name, align_bytes=64)
            nc.sync.dma_start(out=raw[:], in_=rows_of_4(dram))
            return raw

        def load_row_pair(s, u):
            raw = keep.tile([P, 2, T], F32, name=f"x_raw_{s}_{u}", align_bytes=64)
            rows = rows_of_4(xT[s * K_PASS : (s + 1) * K_PASS, :])
            nc.sync.dma_start(out=raw[:], in_=rows[:, 2 * u : 2 * u + 2, :])
            return raw

        offsets = keep.tile([P, S // 16], U16, name="offsets")
        x_raw = [load_row_pair(0, 0)]
        nc.sync.dma_start(offsets[:], offs)
        x_raw.append(load_row_pair(0, 1))
        margin = S - EDGE
        shared = keep.tile([P, 2 * T + 2 * margin], F32, name="x_raw_1_0", align_bytes=64)
        rows = rows_of_4(xT[K_PASS:, :])[:, 0:2, :].rearrange("p j w -> p (j w)")
        nc.sync.dma_start(out=shared[:, margin : margin + 2 * T], in_=rows)
        x_raw.append(shared[:, margin : margin + 2 * T].rearrange("p (j w) -> p j w", j=2))
        x_raw.append(load_row_pair(1, 1))
        w1_raw = [load(w1[s * K_PASS : (s + 1) * K_PASS, :], [P, PACK, H], f"w1_raw_{s}") for s in range(2)]
        w3_raw = load(w3, [P, PACK, H], "w3_raw")
        e_raw = []
        for first, count in EDGE_LOADS:
            raw = load(eT[:, first * CHUNK : (first + count) * CHUNK], [P, PACK, count * CHUNK], f"e_raw_{first}")
            e_raw.extend([raw[:, :, chunk(q)] for q in range(count)])
        w2_raw = load(w2, [P, PACK, N], "w2_raw")

        warm = keep.tile([P, 1], F32, name="warm")
        nc.vector.memset(warm[:], 0.0)
        nc.scalar.activation(out=warm[:], in_=warm[:], func=SIGMOID)

        x_codes = [keep.tile([P, S], U32, name=f"x_codes_{s}", align_bytes=64) for s in range(2)]
        x_scales = [keep.tile([P, S], U8, name=f"x_scales_{s}", align_bytes=64) for s in range(2)]

        def pick_atoms(s):
            words = keep.tile([P, 2, S], U32, name=f"words_{s}", align_bytes=64)
            if s == 0:
                halves = [shared[:, :S], shared[:, 2 * T + 2 * margin - S :]]
            else:
                own = keep.tile([P, 2 * S], F32, name="picked_1", align_bytes=64)
                halves = [own[:, :S], own[:, S:]]
            parts = [slice(0, S // 2), slice(S // 2, S)]
            for u in range(2):
                pairs = keep.tile([P, T, 2], BF16, name=f"pairs_{s}_{u}", align_bytes=64)
                if (s, u) == (1, 0):
                    for cols in (slice(0, EDGE), slice(T - EDGE, T)):
                        round_columns(pairs[:, cols], x_raw[2][:, :, cols], EDGE, 0)
                    round_columns(pairs[:, EDGE : T - EDGE], x_raw[2][:, :, EDGE : T - EDGE], T - 2 * EDGE, T - 2 * EDGE)
                    weave_and_quantize[0]()
                else:
                    round_columns(pairs[:], x_raw[2 * s + u][:], T, X_SCALAR_COLUMNS[2 * s + u])
                window = pairs[:].rearrange("p w e -> p (w e)").bitcast(U32)
                for part in parts:
                    listed = offsets[:, part.start // 16 : part.stop // 16]
                    nc.vector.tensor_copy(out=words[:, u, part], in_=window.indirect(listed))

            def finish():
                for part, half in zip(parts, halves):
                    dst = half.bitcast(I32).rearrange("p (c i u) -> p c u i", i=2, u=2)
                    src = words[:, :, part].bitcast(I32).rearrange("p u (c i) -> p c u i", i=2)
                    nc.vector.tensor_copy(out=dst, in_=src)
                for part, half in zip(parts, halves):
                    quantize(x_codes[s][:, part], x_scales[s][:, part], half.bitcast(BF16))

            weave_and_quantize.append(finish)

        weave_and_quantize = []
        pick_atoms(0)
        pick_atoms(1)
        weave_and_quantize[1]()

        def c_bank_tag(n):
            return f"bank_{n}"

        def f_bank_tag(n):
            return f"bank_{CHUNKS + n}"

        def slot(t):
            return slice(t * P, (t + 1) * P)

        w1_codes = keep.tile([P, 2, H], U32, name="w1_codes", align_bytes=64)
        w1_scales = keep.tile([P, 2, H], U8, name="w1_scales", align_bytes=64)
        c_banks = [psum.tile([P, PACK, CHUNK], F32, name=f"c_{n}", tag=c_bank_tag(n)) for n in range(CHUNKS)]

        def pass_of_c(s, n):
            for t in range(PACK):
                mx_pass(
                    c_banks[n][:, t, :],
                    w1_codes[:, s, slot(t)],
                    w1_scales[:, s, slot(t)],
                    x_codes[s][:, chunk(n)],
                    x_scales[s][:, chunk(n)],
                    start=(s == 0 and t == 0),
                    stop=(s == 1 and t == PACK - 1),
                )

        for s in range(2):
            dealt = keep.tile([P, PACK, P, PACK], BF16, name=f"w1_dealt_{s}", align_bytes=64)
            for h in range(2):
                dst = dealt[:, 2 * h : 2 * h + 2].rearrange("p t m j -> p m j t")
                src = w1_raw[s][:].rearrange("p j (m t) -> p m j t", t=PACK)[:, :, :, 2 * h : 2 * h + 2]
                rows = W1_SCALAR_ROWS[s][h]
                nc.scalar.copy(out=dst[:, :rows], in_=src[:, :rows])
                if rows < P:
                    nc.vector.tensor_copy(out=dst[:, rows:], in_=src[:, rows:])
            for h in range(2):
                cols = slice(2 * h * P, 2 * (h + 1) * P)
                values = dealt[:, 2 * h : 2 * h + 2].rearrange("p t m j -> p (t m j)")
                quantize(w1_codes[:, s, cols], w1_scales[:, s, cols], values)
            for n in range(CHUNKS if s == 0 else 2):
                pass_of_c(s, n)

        w3_codes = keep.tile([P, H], U32, name="w3_codes", align_bytes=64)
        w3_scales = keep.tile([P, H], U8, name="w3_scales", align_bytes=64)
        w3_pairs = [keep.tile([P, 2, P, PACK], BF16, name=f"w3_pair_{h}", align_bytes=64)[:] for h in range(2)]
        w2_codes = keep.tile([P, N], U32, name="w2_codes", align_bytes=64)
        w2_scales = keep.tile([P, N], U8, name="w2_scales", align_bytes=64)
        w2_rounded = keep.tile([P, N, PACK], BF16, name="w2_rounded", align_bytes=64)
        e_rounded, e_codes, e_scales, gates, z_values, z_codes, z_scales = [{} for name in range(7)]

        def round_w3(engine_copy, h, rows):
            raw = w3_raw[:].rearrange("p j (m t) -> p m j t", t=PACK)[:, rows, :, 2 * h : 2 * h + 2]
            engine_copy(out=w3_pairs[h].rearrange("p t m j -> p m j t")[:, rows], in_=raw)

        def quantize_w3(h):
            cols = slice(2 * h * P, 2 * (h + 1) * P)
            quantize(w3_codes[:, cols], w3_scales[:, cols], w3_pairs[h].rearrange("p t m j -> p (t m j)"))

        def round_edges(n):
            e_rounded[n] = keep.tile([P, CHUNK, PACK], BF16, name=f"e_rounded_{n}", tag="e_raw_1" if n == 2 else f"e_rounded_{n}", align_bytes=64)
            round_columns(e_rounded[n][:], e_raw[n], CHUNK, E_SCALAR_COLUMNS[n])

        def quantize_edges(n):
            e_codes[n] = keep.tile([P, CHUNK], U32, name=f"e_codes_{n}", align_bytes=64)
            if n in HELD_BY:
                e_scales[n] = x_scales[1][4:P, chunk(HELD_BY[n])]
            else:
                own = keep.tile([P, CHUNK], U8, name=f"e_scales_{n}", align_bytes=64)
                e_scales[n] = own[:]
            quantize(e_codes[n][:], e_scales[n], e_rounded[n][:].rearrange("p w t -> p (w t)"))

        def f_passes(bank, n, slots):
            for i, t in enumerate(slots):
                mx_pass(bank[:, i, :], w3_codes[:, slot(t)], w3_scales[:, slot(t)], e_codes[n][:], e_scales[n])

        def gate(n):
            f_bank = psum.tile([P, PACK, CHUNK], F32, name=f"f_{n}", tag=f_bank_tag(n))
            f_passes(f_bank, n, range(PACK))
            tile = keep.tile([P, CHUNK, PACK], F32, name=f"gate_{n}", align_bytes=64)
            nc.scalar.activation(out=tile[:], in_=f_bank[:].rearrange("p t n -> p n t"), func=SIGMOID)
            gates[n] = tile[:].rearrange("p n (h e) -> p n h e", e=2)

        first_gate = keep.tile([P, 2, CHUNK, 2], F32, name="gate_0", align_bytes=64)
        gates[0] = first_gate[:].rearrange("p h n e -> p n h e")

        def half_gate(h):
            f_bank = psum.tile([P, 2, CHUNK], F32, name=f"f_0_{h}", tag=f_bank_tag(h * LAST))
            f_passes(f_bank, 0, (2 * h, 2 * h + 1))
            nc.scalar.activation(out=first_gate[:, h], in_=f_bank[:].rearrange("p t n -> p n t"), func=SIGMOID)

        def message(n):
            z_values[n] = keep.tile([P, CHUNK, PACK], BF16, name=f"z_{n}", align_bytes=64)
            c = c_banks[n][:].rearrange("p (h e) n -> p n h e", e=2)
            z = z_values[n][:].rearrange("p n (h e) -> p n h e", e=2)
            nc.vector.tensor_tensor(out=z, in0=c, in1=gates[n], op=MULT)

        def quantize_z(n):
            z_codes[n] = keep.tile([P, CHUNK], U32, name=f"z_codes_{n}", align_bytes=64)
            z_scales[n] = keep.tile([P, CHUNK], U8, name=f"z_scales_{n}", align_bytes=64)
            quantize(z_codes[n][:], z_scales[n][:], z_values[n][:].rearrange("p n t -> p (n t)"))

        result = keep.tile([P, S], F32, name="result")

        def project(n):
            o_bank = psum.tile([P, CHUNK], F32, name=f"o_{n}", tag=f_bank_tag(LAST - n))
            mx_pass(o_bank[:], w2_codes[:], w2_scales[:], z_codes[n][:], z_scales[n][:])
            nc.scalar.copy(out=result[:, chunk(n)], in_=o_bank[:])
            if n > 0:
                cols = slice(0, 2 * CHUNK) if n == 1 else chunk(n)
                nc.sync.dma_start(out=out[:, cols], in_=result[:, cols])

        round_w3(nc.scalar.copy, 0, slice(0, W3_SCALAR_ROWS))
        round_w3(nc.vector.tensor_copy, 0, slice(W3_SCALAR_ROWS, P))
        round_w3(nc.vector.tensor_copy, 1, slice(0, P))
        round_edges(0)
        round_edges(1)
        quantize_w3(0)
        quantize_edges(0)
        half_gate(0)
        quantize_w3(1)
        half_gate(1)
        quantize_edges(1)
        round_edges(2)
        round_edges(LAST)
        gate(1)
        pass_of_c(1, HELD_BY[1])
        quantize_edges(2)
        gate(2)
        message(0)
        quantize_edges(LAST)
        round_columns(w2_rounded[:], w2_raw[:], N, N)
        gate(LAST)
        pass_of_c(1, HELD_BY[LAST])
        message(1)
        quantize_z(0)
        message(2)
        quantize_z(1)
        quantize(w2_codes[:], w2_scales[:], w2_rounded[:].rearrange("p w t -> p (w t)"))
        message(LAST)
        quantize_z(2)
        quantize_z(LAST)
        for n in range(CHUNKS):
            project(n)
